import numpy as np
import ml_dtypes


def mxq(x, axis, fmt="e4m3"):
    dtype, down = {"e4m3": (ml_dtypes.float8_e4m3fn, 7), "e5m2": (ml_dtypes.float8_e5m2, 14)}[fmt]
    v = np.moveaxis(np.asarray(x, np.float32).astype(ml_dtypes.bfloat16).astype(np.float64), axis, -1)
    blocks = v.reshape(v.shape[:-1] + (-1, 32))
    amax = np.abs(blocks).max(-1, keepdims=True)
    byte = np.maximum(np.where(amax > 0, np.frexp(amax)[1] - 1 + 127, 0) - down, 1)
    scale = np.exp2(byte - 127.0)
    codes = (blocks / scale).astype(np.float32).astype(dtype).astype(np.float64)
    return np.moveaxis((codes * scale).reshape(v.shape), -1, axis)


WIDE = False


def mx_kscale(k, group=512):
    if not WIDE:
        return np.ones(k)
    levels = np.array([10, -10, 5, -5, 0])
    if group != 512:
        return np.exp2(np.random.permutation(np.resize(levels, k // group))).repeat(group)
    if k % 512:
        return np.exp2(np.random.permutation(np.resize(levels, k // 32))).repeat(32)
    a = np.empty((k // 512, 16))
    for p in range(k // 512):
        a[p, :8] = np.random.permutation(np.resize(levels, 8))
        for g in range(8):
            far = levels[np.abs(levels - a[p, g]) >= 10]
            a[p, g + 8] = far[np.random.randint(len(far))]
    return np.exp2(a.ravel()).repeat(32)


def f64(x):
    return np.asarray(x).astype(np.float64)


def silu(v):
    return v / (1.0 + np.exp(-v))


def bf(x):
    return np.asarray(x, np.float32).astype(ml_dtypes.bfloat16)


def planes(Y):
    r, m = Y.shape
    b = f64(bf(Y)).reshape(r // 32, 32, m)
    amax = np.abs(b).max(1)
    byte = np.clip(np.where(amax > 0, np.frexp(amax)[1] - 1 + 127 - 7, 1), 1, 254)
    codes = (b * np.exp2(127.0 - byte)[:, None, :]).reshape(r, m).astype(np.float32).astype(ml_dtypes.float8_e4m3fn).view(np.uint8)
    words = codes.reshape(r // 512, 128, 4, m).transpose(0, 1, 3, 2)
    return np.ascontiguousarray(words), np.ascontiguousarray(byte.astype(np.uint8).reshape(r // 512, 16, m))


G, D, M, N = 2, 256, 256, 512


def setup_inputs():
    n = np.random.standard_normal
    s_d = mx_kscale(D, 0)
    return {
        "x": (n((G, D, N)) * s_d[:, None]).astype(np.float32),
        "w": (n((G, D, M)) / np.sqrt(D) / s_d[:, None]).astype(np.float32),
        "u": (n((G, D, M)) / np.sqrt(D) / s_d[:, None]).astype(np.float32),
    }


def reference(x, w, u):
    wq = mxq(f64(w), 1, "e4m3")
    xq = mxq(f64(x), 1, "e4m3")
    zw = wq.transpose(0, 2, 1) @ xq
    uq = mxq(f64(u), 1, "e4m3")
    zu = uq.transpose(0, 2, 1) @ xq
    y = silu(zw) * zu
    Y = y.reshape(G * M, N)
    words, scales = planes(Y)
    return Y, words, scales

@@ -1,0 +1,190 @@
+from contextlib import ExitStack
+
+import concourse.mybir as mybir
+
+G, D, M, N = 2, 256, 256, 512
+FLOPS = 2 * 2 * G * D * M * N
+
+F32 = mybir.dt.float32
+BF16 = mybir.dt.bfloat16
+I32 = mybir.dt.int32
+U32 = mybir.dt.uint32
+U8 = mybir.dt.uint8
+FP8X4 = mybir.dt.float8_e4m3fn_x4
+SILU = mybir.ActivationFunctionType.Silu
+MULT = mybir.AluOpType.mult
+
+P = 128
+PACK = 4
+ROWS = D // PACK
+HALF = P // 2
+NT = 128
+CHUNK = 2 * NT
+CHUNKS = N // CHUNK
+PADDED = HALF + PACK * P
+X_SPLIT = 176
+
+
+def interleave(copy, dst, src, lo, hi):
+    copy(
+        out=dst[:, lo * PACK : hi * PACK].rearrange("p (c i t) -> p c t i", i=4, t=PACK),
+        in_=src[:, :, lo:hi].rearrange("p t (c i) -> p c t i", i=4),
+    )
+
+
+def tile_rows_pl_gswiglu_kernel(tc, x, w, u, out_0, out_1, out_2):
+    nc = tc.nc
+    with ExitStack() as ctx:
+        sb = ctx.enter_context(tc.tile_pool(name="sb", bufs=1))
+        ps = ctx.enter_context(tc.psum_pool(name="ps", bufs=1))
+        ctx.enter_context(tc.manual_schedule())
+
+        x_rows = x.rearrange("g (p j) n -> (g p) j n", j=PACK)
+        raw = {}
+
+        def load_weight(name, src):
+            t = sb.tile([P, PACK, M], F32, name=name + "_raw")
+            nc.sync.dma_start(out=t[:], in_=src.rearrange("g (p j) m -> (g p) j m", j=PACK))
+            raw[name] = t
+
+        def load_x(c):
+            t = sb.tile([P, PACK, CHUNK], F32, name="x_raw%d" % c)
+            nc.sync.dma_start(out=t[:], in_=x_rows[:, :, c * CHUNK : (c + 1) * CHUNK])
+            raw[c] = t
+
+        load_weight("w", w)
+        load_x(0)
+        load_weight("u", u)
+        load_x(1)
+
+        codes, scales = {}, {}
+        for name in ("w", "u"):
+            codes[name] = sb.tile([P, PADDED], U32, name=name + "_codes", align_bytes=64)
+            scales[name] = sb.tile([P, PADDED], U8, name=name + "_scales", align_bytes=64)
+            nc.vector.memset(codes[name][:], 0)
+            nc.vector.memset(scales[name][:].bitcast(U32), 0)
+
+        warm = sb.tile([P, 8], F32, name="warm")
+        warm2 = sb.tile([P, 8], F32, name="warm2")
+        nc.vector.memset(warm[:], 0.0)
+        nc.scalar.activation(out=warm2[:], in_=warm[:], func=SILU)
+
+        def prep_weight(name):
+            dealt = sb.tile([P, PACK * M], BF16, name=name + "_bf", align_bytes=64)
+            src = raw[name][:].rearrange("p j (q z) -> p q z j", z=PACK)
+            dst = dealt[:].rearrange("p (z q j) -> p q z j", z=PACK, j=PACK)
+            nc.vector.tensor_copy(out=dst[:, :, 0:3, :], in_=src[:, :, 0:3, :])
+            nc.scalar.copy(out=dst[:, :, 3, :], in_=src[:, :, 3, :])
+            for z in (3, 0, 1, 2):
+                win = slice(HALF + P * z, P + P * z)
+                nc.vector.quantize_mx(
+                    out=codes[name][:, win].bitcast(FP8X4),
+                    scales=scales[name][:, win],
+                    in_=dealt[:, z * M : (z + 1) * M],
+                )
+
+        def prep_x(c, share):
+            grouped = sb.tile([P, CHUNK * PACK], BF16, name="x_bf%d" % c, align_bytes=64)
+            codes[c] = sb.tile([P, CHUNK], U32, name="x_codes%d" % c, align_bytes=64)
+            scales[c] = sb.tile([P, CHUNK], U8, name="x_scales%d" % c, align_bytes=64)
+            interleave(nc.vector.tensor_copy, grouped, raw[c], 0, NT)
+            interleave(nc.vector.tensor_copy, grouped, raw[c], NT, share)
+            if share < CHUNK:
+                interleave(nc.scalar.copy, grouped, raw[c], share, CHUNK)
+            for h in range(2):
+                cols = slice(h * NT, (h + 1) * NT)
+                nc.vector.quantize_mx(
+                    out=codes[c][:, cols].bitcast(FP8X4),
+                    scales=scales[c][:, cols],
+                    in_=grouped[:, h * NT * PACK : (h + 1) * NT * PACK],
+                )
+
+        sums = {}
+
+        def products(name, c):
+            for g in range(G):
+                sums[name, c, g] = ps.tile([P, PACK * NT], F32, name="z_%s%d%d" % (name, c, g))
+            for z in range(PACK):
+                for h in range(2):
+                    start = P * z + HALF * (1 - h)
+                    wcols = slice(start, start + P)
+                    xcols = slice(h * NT, (h + 1) * NT)
+                    for g in range(G):
+                        rows = slice(g * ROWS, (g + 1) * ROWS)
+                        nc.tensor.matmul_mx(
+                            out=sums[name, c, g][:, z * NT : (z + 1) * NT],
+                            lhsT=codes[name][rows, wcols].bitcast(FP8X4),
+                            lhsT_scale=scales[name][rows, wcols],
+                            rhs=codes[c][rows, xcols].bitcast(FP8X4),
+                            rhs_scale=scales[c][rows, xcols],
+                            start=(h == 0),
+                            stop=(h == 1),
+                        )
+
+        gates, ys, y_bf, y_codes, y_scales = {}, {}, {}, {}, {}
+        for c in range(CHUNKS):
+            y_codes[c] = sb.tile([P, G * NT], U32, name="y_codes%d" % c, align_bytes=64)
+            y_scales[c] = sb.tile([P, G * NT], U8, name="y_scales%d" % c, align_bytes=64)
+
+        def gate(c, g):
+            gates[c, g] = sb.tile([P, PACK * NT], F32, name="gate%d%d" % (c, g))
+            nc.scalar.activation(out=gates[c, g][:], in_=sums["w", c, g][:], func=SILU)
+
+        def multiply(c, g):
+            ys[c, g] = sb.tile([P, PACK, NT], F32, name="y%d%d" % (c, g))
+            nc.vector.tensor_tensor(
+                out=ys[c, g][:].rearrange("p z n -> p (z n)"), in0=sums["u", c, g][:], in1=gates[c, g][:], op=MULT
+            )
+            rows = out_0[g * M : (g + 1) * M, :].rearrange("(p z) n -> p z n", z=PACK)
+            for h in range(2):
+                col = c * CHUNK + h * NT
+                nc.sync.dma_start(out=rows[:, :, col : col + NT], in_=ys[c, g][h * HALF : (h + 1) * HALF])
+
+        def round_y(copy, c, g):
+            y_bf[c, g] = sb.tile([P, NT * PACK], BF16, name="y_bf%d%d" % (c, g), align_bytes=64)
+            interleave(copy, y_bf[c, g], ys[c, g], 0, NT)
+
+        def quantize_y(c, g):
+            cols = slice(g * NT, (g + 1) * NT)
+            nc.vector.quantize_mx(out=y_codes[c][:, cols].bitcast(FP8X4), scales=y_scales[c][:, cols], in_=y_bf[c, g][:])
+
+        words_out = out_1[0].rearrange("p n t -> p (n t)").bitcast(I32).rearrange("(g p) n -> p g n", g=G)
+        scales_out = out_2[0].bitcast(I32).rearrange("(g b r) n -> b r g n", g=G, b=2)
+
+        def store_planes(c, scale_queue):
+            words = y_codes[c][:].bitcast(I32).rearrange("p (g n) -> p g n", g=G)
+            for h in range(2):
+                col = c * CHUNK + h * NT
+                nc.sync.dma_start(out=words_out[:, :, col : col + NT], in_=words[h * HALF : (h + 1) * HALF])
+            rows = y_scales[c][:].bitcast(I32).rearrange("p (g n) -> p g n", g=G)
+            for q in range(4):
+                h, b = divmod(q, 2)
+                col = (c * CHUNK + h * NT) // 4
+                scale_queue.dma_start(out=scales_out[b][:, :, col : col + NT // 4], in_=rows[32 * q : 32 * q + 4])
+
+        prep_weight("w")
+        prep_x(0, X_SPLIT)
+        products("w", 0)
+        prep_weight("u")
+        products("u", 0)
+        prep_x(1, CHUNK)
+        products("w", 1)
+        products("u", 1)
+        gate(0, 0)
+        gate(0, 1)
+        multiply(0, 0)
+        multiply(0, 1)
+        round_y(nc.scalar.copy, 0, 0)
+        gate(1, 0)
+        gate(1, 1)
+        round_y(nc.vector.tensor_copy, 0, 1)
+        quantize_y(0, 0)
+        quantize_y(0, 1)
+        store_planes(0, nc.gpsimd)
+        multiply(1, 0)
+        multiply(1, 1)
+        round_y(nc.scalar.copy, 1, 0)
+        round_y(nc.vector.tensor_copy, 1, 1)
+        quantize_y(1, 0)
+        quantize_y(1, 1)
+        store_planes(1, nc.scalar)

@@ -135,10 +135,14 @@ def tile_rows_pl_gswiglu_kernel(tc, x, w, u, out_0, out_1, out_2):
             nc.vector.tensor_tensor(
                 out=ys[c, g][:].rearrange("p z n -> p (z n)"), in0=sums["u", c, g][:], in1=gates[c, g][:], op=MULT
             )
+
+        queues = (nc.sync, nc.scalar)
+
+        def store_y(c, g):
             rows = out_0[g * M : (g + 1) * M, :].rearrange("(p z) n -> p z n", z=PACK)
             for h in range(2):
                 col = c * CHUNK + h * NT
-                nc.sync.dma_start(out=rows[:, :, col : col + NT], in_=ys[c, g][h * HALF : (h + 1) * HALF])
+                queues[h].dma_start(out=rows[:, :, col : col + NT], in_=ys[c, g][h * HALF : (h + 1) * HALF])
 
         def round_y(copy, c, g):
             y_bf[c, g] = sb.tile([P, NT * PACK], BF16, name="y_bf%d%d" % (c, g), align_bytes=64)
@@ -151,16 +155,16 @@ def tile_rows_pl_gswiglu_kernel(tc, x, w, u, out_0, out_1, out_2):
         words_out = out_1[0].rearrange("p n t -> p (n t)").bitcast(I32).rearrange("(g p) n -> p g n", g=G)
         scales_out = out_2[0].bitcast(I32).rearrange("(g b r) n -> b r g n", g=G, b=2)
 
-        def store_planes(c, scale_queue):
+        def store_planes(c):
             words = y_codes[c][:].bitcast(I32).rearrange("p (g n) -> p g n", g=G)
             for h in range(2):
                 col = c * CHUNK + h * NT
-                nc.sync.dma_start(out=words_out[:, :, col : col + NT], in_=words[h * HALF : (h + 1) * HALF])
+                queues[h].dma_start(out=words_out[:, :, col : col + NT], in_=words[h * HALF : (h + 1) * HALF])
             rows = y_scales[c][:].bitcast(I32).rearrange("p (g n) -> p g n", g=G)
             for q in range(4):
                 h, b = divmod(q, 2)
                 col = (c * CHUNK + h * NT) // 4
-                scale_queue.dma_start(out=scales_out[b][:, :, col : col + NT // 4], in_=rows[32 * q : 32 * q + 4])
+                queues[h].dma_start(out=scales_out[b][:, :, col : col + NT // 4], in_=rows[32 * q : 32 * q + 4])
 
         prep_weight("w")
         prep_x(0, X_SPLIT)
@@ -174,17 +178,21 @@ def tile_rows_pl_gswiglu_kernel(tc, x, w, u, out_0, out_1, out_2):
         gate(0, 1)
         multiply(0, 0)
         multiply(0, 1)
+        store_y(0, 0)
         round_y(nc.scalar.copy, 0, 0)
+        store_y(0, 1)
         gate(1, 0)
         gate(1, 1)
         round_y(nc.vector.tensor_copy, 0, 1)
         quantize_y(0, 0)
         quantize_y(0, 1)
-        store_planes(0, nc.gpsimd)
+        store_planes(0)
         multiply(1, 0)
         multiply(1, 1)
+        store_y(1, 0)
         round_y(nc.scalar.copy, 1, 0)
+        store_y(1, 1)
         round_y(nc.vector.tensor_copy, 1, 1)
         quantize_y(1, 0)
         quantize_y(1, 1)
-        store_planes(1, nc.scalar)
+        store_planes(1)

@@ -58,6 +58,26 @@ def tile_rows_pl_gswiglu_kernel(tc, x, w, u, out_0, out_1, out_2):
         load_x(1)
 
         codes, scales = {}, {}
+        ones = sb.tile([P, NT * PACK], BF16, name="ones", align_bytes=64)
+        ones_codes = sb.tile([P, NT], U32, name="ones_codes", align_bytes=64)
+        ones_scales = sb.tile([P, NT], U8, name="ones_scales", align_bytes=64)
+        spare = ps.tile([P, PACK * NT], F32, name="spare")
+        nc.vector.memset(ones[:], 1.0)
+        nc.vector.quantize_mx(out=ones_codes[:].bitcast(FP8X4), scales=ones_scales[:], in_=ones[:])
+
+        def warm_tensor(count, lhs_codes, lhs_scales):
+            for k in range(count):
+                nc.tensor.matmul_mx(
+                    out=spare[:, (k % PACK) * NT : (k % PACK + 1) * NT],
+                    lhsT=lhs_codes.bitcast(FP8X4),
+                    lhsT_scale=lhs_scales,
+                    rhs=ones_codes[:].bitcast(FP8X4),
+                    rhs_scale=ones_scales[:],
+                    start=True,
+                    stop=True,
+                )
+
+        warm_tensor(28, ones_codes[:], ones_scales[:])
         for name in ("w", "u"):
             codes[name] = sb.tile([P, PADDED], U32, name=name + "_codes", align_bytes=64)
             scales[name] = sb.tile([P, PADDED], U8, name=name + "_scales", align_bytes=64)
@@ -99,27 +119,30 @@ def tile_rows_pl_gswiglu_kernel(tc, x, w, u, out_0, out_1, out_2):
                     in_=grouped[:, h * NT * PACK : (h + 1) * NT * PACK],
                 )
 
+        banks = {(k, g): ps.tile([P, PACK * NT], F32, name="bank%d%d" % (k, g)) for k in range(3) for g in range(G)}
         sums = {}
+        for g in range(G):
+            sums["w", 0, g] = banks[0, g]
+            sums["u", 0, g] = banks[1, g]
+            sums["w", 1, g] = banks[2, g]
+            sums["u", 1, g] = banks[0, g]
 
-        def products(name, c):
-            for g in range(G):
-                sums[name, c, g] = ps.tile([P, PACK * NT], F32, name="z_%s%d%d" % (name, c, g))
+        def products(name, c, g):
+            rows = slice(g * ROWS, (g + 1) * ROWS)
             for z in range(PACK):
                 for h in range(2):
                     start = P * z + HALF * (1 - h)
                     wcols = slice(start, start + P)
                     xcols = slice(h * NT, (h + 1) * NT)
-                    for g in range(G):
-                        rows = slice(g * ROWS, (g + 1) * ROWS)
-                        nc.tensor.matmul_mx(
-                            out=sums[name, c, g][:, z * NT : (z + 1) * NT],
-                            lhsT=codes[name][rows, wcols].bitcast(FP8X4),
-                            lhsT_scale=scales[name][rows, wcols],
-                            rhs=codes[c][rows, xcols].bitcast(FP8X4),
-                            rhs_scale=scales[c][rows, xcols],
-                            start=(h == 0),
-                            stop=(h == 1),
-                        )
+                    nc.tensor.matmul_mx(
+                        out=sums[name, c, g][:, z * NT : (z + 1) * NT],
+                        lhsT=codes[name][rows, wcols].bitcast(FP8X4),
+                        lhsT_scale=scales[name][rows, wcols],
+                        rhs=codes[c][rows, xcols].bitcast(FP8X4),
+                        rhs_scale=scales[c][rows, xcols],
+                        start=(h == 0),
+                        stop=(h == 1),
+                    )
 
         gates, ys, y_bf, y_codes, y_scales = {}, {}, {}, {}, {}
         for c in range(CHUNKS):
@@ -167,15 +190,19 @@ def tile_rows_pl_gswiglu_kernel(tc, x, w, u, out_0, out_1, out_2):
                 queues[h].dma_start(out=scales_out[b][:, :, col : col + NT // 4], in_=rows[32 * q : 32 * q + 4])
 
         prep_weight("w")
+        warm_tensor(10, codes["w"][:, 0:P], scales["w"][:, 0:P])
         prep_x(0, X_SPLIT)
-        products("w", 0)
+        products("w", 0, 0)
+        products("w", 0, 1)
         prep_weight("u")
-        products("u", 0)
+        products("u", 0, 0)
+        products("u", 0, 1)
         prep_x(1, CHUNK)
-        products("w", 1)
-        products("u", 1)
         gate(0, 0)
         gate(0, 1)
+        for g in range(G):
+            products("w", 1, g)
+            products("u", 1, g)
         multiply(0, 0)
         multiply(0, 1)
         store_y(0, 0)
@@ -192,7 +219,7 @@ def tile_rows_pl_gswiglu_kernel(tc, x, w, u, out_0, out_1, out_2):
         store_y(1, 0)
         round_y(nc.scalar.copy, 1, 0)
         store_y(1, 1)
-        round_y(nc.vector.tensor_copy, 1, 1)
         quantize_y(1, 0)
+        round_y(nc.vector.tensor_copy, 1, 1)
         quantize_y(1, 1)
         store_planes(1)

@@ -43,56 +43,38 @@ def tile_rows_pl_gswiglu_kernel(tc, x, w, u, out_0, out_1, out_2):
         raw = {}
 
         def load_weight(name, src):
-            t = sb.tile([P, PACK, M], F32, name=name + "_raw")
-            nc.sync.dma_start(out=t[:], in_=src.rearrange("g (p j) m -> (g p) j m", j=PACK))
-            raw[name] = t
+            raw[name] = sb.tile([P, PACK, M], F32, name=name + "_raw")
+            nc.sync.dma_start(out=raw[name][:], in_=src.rearrange("g (p j) m -> (g p) j m", j=PACK))
 
         def load_x(c):
-            t = sb.tile([P, PACK, CHUNK], F32, name="x_raw%d" % c)
-            nc.sync.dma_start(out=t[:], in_=x_rows[:, :, c * CHUNK : (c + 1) * CHUNK])
-            raw[c] = t
+            raw[c] = sb.tile([P, PACK, CHUNK], F32, name="x_raw%d" % c)
+            nc.sync.dma_start(out=raw[c][:], in_=x_rows[:, :, c * CHUNK : (c + 1) * CHUNK])
 
         load_weight("w", w)
         load_x(0)
         load_weight("u", u)
         load_x(1)
 
-        codes, scales = {}, {}
-        ones = sb.tile([P, NT * PACK], BF16, name="ones", align_bytes=64)
-        ones_codes = sb.tile([P, NT], U32, name="ones_codes", align_bytes=64)
-        ones_scales = sb.tile([P, NT], U8, name="ones_scales", align_bytes=64)
-        spare = ps.tile([P, PACK * NT], F32, name="spare")
-        nc.vector.memset(ones[:], 1.0)
-        nc.vector.quantize_mx(out=ones_codes[:].bitcast(FP8X4), scales=ones_scales[:], in_=ones[:])
-
-        def warm_tensor(count, lhs_codes, lhs_scales):
-            for k in range(count):
-                nc.tensor.matmul_mx(
-                    out=spare[:, (k % PACK) * NT : (k % PACK + 1) * NT],
-                    lhsT=lhs_codes.bitcast(FP8X4),
-                    lhsT_scale=lhs_scales,
-                    rhs=ones_codes[:].bitcast(FP8X4),
-                    rhs_scale=ones_scales[:],
-                    start=True,
-                    stop=True,
-                )
-
-        warm_tensor(28, ones_codes[:], ones_scales[:])
-        for name in ("w", "u"):
-            codes[name] = sb.tile([P, PADDED], U32, name=name + "_codes", align_bytes=64)
-            scales[name] = sb.tile([P, PADDED], U8, name=name + "_scales", align_bytes=64)
-            nc.vector.memset(codes[name][:], 0)
-            nc.vector.memset(scales[name][:].bitcast(U32), 0)
-
         warm = sb.tile([P, 8], F32, name="warm")
         warm2 = sb.tile([P, 8], F32, name="warm2")
         nc.vector.memset(warm[:], 0.0)
         nc.scalar.activation(out=warm2[:], in_=warm[:], func=SILU)
 
+        codes, scales, grouped = {}, {}, {}
+        for name in ("w", "u"):
+            codes[name] = sb.tile([P, PADDED], U32, name=name + "_codes", align_bytes=64)
+            scales[name] = sb.tile([P, PADDED], U8, name=name + "_scales", align_bytes=64)
+            grouped[name] = sb.tile([P, PACK * M], BF16, name=name + "_bf", align_bytes=64)
+            nc.vector.memset(codes[name][:], 0)
+            nc.vector.memset(scales[name][:].bitcast(U32), 0)
+        for c in range(CHUNKS):
+            grouped[c] = sb.tile([P, CHUNK * PACK], BF16, name="x_bf%d" % c, align_bytes=64)
+            codes[c] = sb.tile([P, CHUNK], U32, name="x_codes%d" % c, align_bytes=64)
+            scales[c] = sb.tile([P, CHUNK], U8, name="x_scales%d" % c, align_bytes=64)
+
         def prep_weight(name):
-            dealt = sb.tile([P, PACK * M], BF16, name=name + "_bf", align_bytes=64)
             src = raw[name][:].rearrange("p j (q z) -> p q z j", z=PACK)
-            dst = dealt[:].rearrange("p (z q j) -> p q z j", z=PACK, j=PACK)
+            dst = grouped[name][:].rearrange("p (z q j) -> p q z j", z=PACK, j=PACK)
             nc.vector.tensor_copy(out=dst[:, :, 0:3, :], in_=src[:, :, 0:3, :])
             nc.scalar.copy(out=dst[:, :, 3, :], in_=src[:, :, 3, :])
             for z in (3, 0, 1, 2):
@@ -100,126 +82,112 @@ def tile_rows_pl_gswiglu_kernel(tc, x, w, u, out_0, out_1, out_2):
                 nc.vector.quantize_mx(
                     out=codes[name][:, win].bitcast(FP8X4),
                     scales=scales[name][:, win],
-                    in_=dealt[:, z * M : (z + 1) * M],
+                    in_=grouped[name][:, z * M : (z + 1) * M],
                 )
 
         def prep_x(c, share):
-            grouped = sb.tile([P, CHUNK * PACK], BF16, name="x_bf%d" % c, align_bytes=64)
-            codes[c] = sb.tile([P, CHUNK], U32, name="x_codes%d" % c, align_bytes=64)
-            scales[c] = sb.tile([P, CHUNK], U8, name="x_scales%d" % c, align_bytes=64)
-            interleave(nc.vector.tensor_copy, grouped, raw[c], 0, NT)
-            interleave(nc.vector.tensor_copy, grouped, raw[c], NT, share)
+            interleave(nc.vector.tensor_copy, grouped[c], raw[c], 0, share)
             if share < CHUNK:
-                interleave(nc.scalar.copy, grouped, raw[c], share, CHUNK)
-            for h in range(2):
-                cols = slice(h * NT, (h + 1) * NT)
-                nc.vector.quantize_mx(
-                    out=codes[c][:, cols].bitcast(FP8X4),
-                    scales=scales[c][:, cols],
-                    in_=grouped[:, h * NT * PACK : (h + 1) * NT * PACK],
-                )
+                interleave(nc.scalar.copy, grouped[c], raw[c], share, CHUNK)
+            nc.vector.quantize_mx(out=codes[c][:].bitcast(FP8X4), scales=scales[c][:], in_=grouped[c][:])
 
-        banks = {(k, g): ps.tile([P, PACK * NT], F32, name="bank%d%d" % (k, g)) for k in range(3) for g in range(G)}
         sums = {}
-        for g in range(G):
-            sums["w", 0, g] = banks[0, g]
-            sums["u", 0, g] = banks[1, g]
-            sums["w", 1, g] = banks[2, g]
-            sums["u", 1, g] = banks[0, g]
+        for c in range(CHUNKS):
+            for name in ("w", "u"):
+                for g in range(G):
+                    sums[name, c, g] = ps.tile([P, PACK * NT], F32, name="sums_%s%d%d" % (name, c, g))
 
-        def products(name, c, g):
-            rows = slice(g * ROWS, (g + 1) * ROWS)
-            for z in range(PACK):
+        def products(name, c):
+            for z in (3, 0, 1, 2):
                 for h in range(2):
                     start = P * z + HALF * (1 - h)
                     wcols = slice(start, start + P)
                     xcols = slice(h * NT, (h + 1) * NT)
-                    nc.tensor.matmul_mx(
-                        out=sums[name, c, g][:, z * NT : (z + 1) * NT],
-                        lhsT=codes[name][rows, wcols].bitcast(FP8X4),
-                        lhsT_scale=scales[name][rows, wcols],
-                        rhs=codes[c][rows, xcols].bitcast(FP8X4),
-                        rhs_scale=scales[c][rows, xcols],
-                        start=(h == 0),
-                        stop=(h == 1),
-                    )
+                    for g in range(G):
+                        rows = slice(g * ROWS, (g + 1) * ROWS)
+                        nc.tensor.matmul_mx(
+                            out=sums[name, c, g][:, z * NT : (z + 1) * NT],
+                            lhsT=codes[name][rows, wcols].bitcast(FP8X4),
+                            lhsT_scale=scales[name][rows, wcols],
+                            rhs=codes[c][rows, xcols].bitcast(FP8X4),
+                            rhs_scale=scales[c][rows, xcols],
+                            start=(h == 0),
+                            stop=(h == 1),
+                        )
 
-        gates, ys, y_bf, y_codes, y_scales = {}, {}, {}, {}, {}
+        gates, ys, y_bf = {}, {}, {}
+        y_codes = sb.tile([P, CHUNKS * G * NT], U32, name="y_codes", align_bytes=64)
+        y_scales = sb.tile([P, CHUNKS * G * NT], U8, name="y_scales", align_bytes=64)
         for c in range(CHUNKS):
-            y_codes[c] = sb.tile([P, G * NT], U32, name="y_codes%d" % c, align_bytes=64)
-            y_scales[c] = sb.tile([P, G * NT], U8, name="y_scales%d" % c, align_bytes=64)
+            ys[c] = sb.tile([P, PACK, G, NT], F32, name="y%d" % c)
+            y_bf[c] = sb.tile([P, G * NT * PACK], BF16, name="y_bf%d" % c, align_bytes=64)
 
         def gate(c, g):
             gates[c, g] = sb.tile([P, PACK * NT], F32, name="gate%d%d" % (c, g))
             nc.scalar.activation(out=gates[c, g][:], in_=sums["w", c, g][:], func=SILU)
 
         def multiply(c, g):
-            ys[c, g] = sb.tile([P, PACK, NT], F32, name="y%d%d" % (c, g))
             nc.vector.tensor_tensor(
-                out=ys[c, g][:].rearrange("p z n -> p (z n)"), in0=sums["u", c, g][:], in1=gates[c, g][:], op=MULT
+                out=ys[c][:, :, g, :],
+                in0=sums["u", c, g][:].rearrange("p (z n) -> p z n", z=PACK),
+                in1=gates[c, g][:].rearrange("p (z n) -> p z n", z=PACK),
+                op=MULT,
             )
 
         queues = (nc.sync, nc.scalar)
+        y_out = out_0.rearrange("(g r) (c h n) -> c h r g n", g=G, c=CHUNKS, h=2)
+        words_out = out_1[0].rearrange("p n t -> p (n t)").bitcast(I32)
+        words_out = words_out.rearrange("(g p) (c h n) -> h (p c) g n", g=G, c=CHUNKS, h=2)
+        scales_out = out_2[0].bitcast(I32).rearrange("(g b r) (c h n) -> h b (r c) g n", g=G, b=2, c=CHUNKS, h=2)
 
-        def store_y(c, g):
-            rows = out_0[g * M : (g + 1) * M, :].rearrange("(p z) n -> p z n", z=PACK)
-            for h in range(2):
-                col = c * CHUNK + h * NT
-                queues[h].dma_start(out=rows[:, :, col : col + NT], in_=ys[c, g][h * HALF : (h + 1) * HALF])
+        def store_y(c, h, lo, hi):
+            queues[h].dma_start(out=y_out[c][h][:, lo:hi, :], in_=ys[c][h * HALF : (h + 1) * HALF, :, lo:hi, :])
 
         def round_y(copy, c, g):
-            y_bf[c, g] = sb.tile([P, NT * PACK], BF16, name="y_bf%d%d" % (c, g), align_bytes=64)
-            interleave(copy, y_bf[c, g], ys[c, g], 0, NT)
+            interleave(copy, y_bf[c][:, g * NT * PACK : (g + 1) * NT * PACK], ys[c][:, :, g, :], 0, NT)
 
-        def quantize_y(c, g):
-            cols = slice(g * NT, (g + 1) * NT)
-            nc.vector.quantize_mx(out=y_codes[c][:, cols].bitcast(FP8X4), scales=y_scales[c][:, cols], in_=y_bf[c, g][:])
+        def quantize_y(c, lo, hi):
+            cols = slice((c * G + lo) * NT, (c * G + hi) * NT)
+            nc.vector.quantize_mx(
+                out=y_codes[:, cols].bitcast(FP8X4),
+                scales=y_scales[:, cols],
+                in_=y_bf[c][:, lo * NT * PACK : hi * NT * PACK],
+            )
 
-        words_out = out_1[0].rearrange("p n t -> p (n t)").bitcast(I32).rearrange("(g p) n -> p g n", g=G)
-        scales_out = out_2[0].bitcast(I32).rearrange("(g b r) n -> b r g n", g=G, b=2)
-
-        def store_planes(c):
-            words = y_codes[c][:].bitcast(I32).rearrange("p (g n) -> p g n", g=G)
-            for h in range(2):
-                col = c * CHUNK + h * NT
-                queues[h].dma_start(out=words_out[:, :, col : col + NT], in_=words[h * HALF : (h + 1) * HALF])
-            rows = y_scales[c][:].bitcast(I32).rearrange("p (g n) -> p g n", g=G)
-            for q in range(4):
-                h, b = divmod(q, 2)
-                col = (c * CHUNK + h * NT) // 4
-                queues[h].dma_start(out=scales_out[b][:, :, col : col + NT // 4], in_=rows[32 * q : 32 * q + 4])
+        def store_planes(h):
+            queues[h].dma_start(out=words_out[h], in_=y_codes[h * HALF : (h + 1) * HALF, :].bitcast(I32))
+            for b in range(2):
+                first = h * HALF + 32 * b
+                queues[h].dma_start(out=scales_out[h][b], in_=y_scales[first : first + 4, :].bitcast(I32))
 
         prep_weight("w")
-        warm_tensor(10, codes["w"][:, 0:P], scales["w"][:, 0:P])
         prep_x(0, X_SPLIT)
-        products("w", 0, 0)
-        products("w", 0, 1)
+        products("w", 0)
         prep_weight("u")
-        products("u", 0, 0)
-        products("u", 0, 1)
+        products("u", 0)
         prep_x(1, CHUNK)
         gate(0, 0)
         gate(0, 1)
-        for g in range(G):
-            products("w", 1, g)
-            products("u", 1, g)
+        products("w", 1)
+        products("u", 1)
         multiply(0, 0)
         multiply(0, 1)
-        store_y(0, 0)
-        round_y(nc.scalar.copy, 0, 0)
-        store_y(0, 1)
+        store_y(0, 0, 0, 1)
+        store_y(0, 1, 0, 1)
         gate(1, 0)
+        store_y(0, 0, 1, 2)
+        store_y(0, 1, 1, 2)
         gate(1, 1)
-        round_y(nc.vector.tensor_copy, 0, 1)
-        quantize_y(0, 0)
-        quantize_y(0, 1)
-        store_planes(0)
+        round_y(nc.vector.tensor_copy, 0, 0)
+        round_y(nc.scalar.copy, 0, 1)
         multiply(1, 0)
         multiply(1, 1)
-        store_y(1, 0)
         round_y(nc.scalar.copy, 1, 0)
-        store_y(1, 1)
-        quantize_y(1, 0)
+        store_y(1, 0, 0, G)
+        store_y(1, 1, 0, G)
+        quantize_y(0, 0, 1)
         round_y(nc.vector.tensor_copy, 1, 1)
-        quantize_y(1, 1)
-        store_planes(1)
+        quantize_y(0, 1, 2)
+        quantize_y(1, 0, G)
+        for h in range(2):
+            store_planes(h)

@@ -21,6 +21,7 @@ HALF = P // 2
 NT = 128
 CHUNK = 2 * NT
 CHUNKS = N // CHUNK
+BANK = PACK * NT
 PADDED = HALF + PACK * P
 X_SPLIT = 176
 
@@ -50,8 +51,8 @@ def tile_rows_pl_gswiglu_kernel(tc, x, w, u, out_0, out_1, out_2):
             raw[c] = sb.tile([P, PACK, CHUNK], F32, name="x_raw%d" % c)
             nc.sync.dma_start(out=raw[c][:], in_=x_rows[:, :, c * CHUNK : (c + 1) * CHUNK])
 
-        load_weight("w", w)
         load_x(0)
+        load_weight("w", w)
         load_weight("u", u)
         load_x(1)
 
@@ -60,11 +61,11 @@ def tile_rows_pl_gswiglu_kernel(tc, x, w, u, out_0, out_1, out_2):
         nc.vector.memset(warm[:], 0.0)
         nc.scalar.activation(out=warm2[:], in_=warm[:], func=SILU)
 
-        codes, scales, grouped = {}, {}, {}
+        grouped, codes, scales = {}, {}, {}
         for name in ("w", "u"):
+            grouped[name] = sb.tile([P, PACK * M], BF16, name=name + "_bf", align_bytes=64)
             codes[name] = sb.tile([P, PADDED], U32, name=name + "_codes", align_bytes=64)
             scales[name] = sb.tile([P, PADDED], U8, name=name + "_scales", align_bytes=64)
-            grouped[name] = sb.tile([P, PACK * M], BF16, name=name + "_bf", align_bytes=64)
             nc.vector.memset(codes[name][:], 0)
             nc.vector.memset(scales[name][:].bitcast(U32), 0)
         for c in range(CHUNKS):
@@ -75,9 +76,9 @@ def tile_rows_pl_gswiglu_kernel(tc, x, w, u, out_0, out_1, out_2):
         def prep_weight(name):
             src = raw[name][:].rearrange("p j (q z) -> p q z j", z=PACK)
             dst = grouped[name][:].rearrange("p (z q j) -> p q z j", z=PACK, j=PACK)
-            nc.vector.tensor_copy(out=dst[:, :, 0:3, :], in_=src[:, :, 0:3, :])
-            nc.scalar.copy(out=dst[:, :, 3, :], in_=src[:, :, 3, :])
-            for z in (3, 0, 1, 2):
+            nc.vector.tensor_copy(out=dst[:, :, 0:2, :], in_=src[:, :, 0:2, :])
+            nc.scalar.copy(out=dst[:, :, 2:PACK, :], in_=src[:, :, 2:PACK, :])
+            for z in range(PACK):
                 win = slice(HALF + P * z, P + P * z)
                 nc.vector.quantize_mx(
                     out=codes[name][:, win].bitcast(FP8X4),
@@ -91,22 +92,18 @@ def tile_rows_pl_gswiglu_kernel(tc, x, w, u, out_0, out_1, out_2):
                 interleave(nc.scalar.copy, grouped[c], raw[c], share, CHUNK)
             nc.vector.quantize_mx(out=codes[c][:].bitcast(FP8X4), scales=scales[c][:], in_=grouped[c][:])
 
-        sums = {}
-        for c in range(CHUNKS):
-            for name in ("w", "u"):
-                for g in range(G):
-                    sums[name, c, g] = ps.tile([P, PACK * NT], F32, name="sums_%s%d%d" % (name, c, g))
+        banks = [[ps.tile([P, BANK], F32, name="bank%d%d" % (g, k)) for k in range(4)] for g in range(G)]
 
-        def products(name, c):
-            for z in (3, 0, 1, 2):
+        def products(name, c, bank, places):
+            for z in places:
                 for h in range(2):
-                    start = P * z + HALF * (1 - h)
-                    wcols = slice(start, start + P)
+                    first = P * z + HALF * (1 - h)
+                    wcols = slice(first, first + P)
                     xcols = slice(h * NT, (h + 1) * NT)
                     for g in range(G):
                         rows = slice(g * ROWS, (g + 1) * ROWS)
                         nc.tensor.matmul_mx(
-                            out=sums[name, c, g][:, z * NT : (z + 1) * NT],
+                            out=banks[g][bank][:, z * NT : (z + 1) * NT],
                             lhsT=codes[name][rows, wcols].bitcast(FP8X4),
                             lhsT_scale=scales[name][rows, wcols],
                             rhs=codes[c][rows, xcols].bitcast(FP8X4),
@@ -115,79 +112,93 @@ def tile_rows_pl_gswiglu_kernel(tc, x, w, u, out_0, out_1, out_2):
                             stop=(h == 1),
                         )
 
-        gates, ys, y_bf = {}, {}, {}
+        gates, y_bf = {}, {}
+        y_first = sb.tile([P, PACK, G, NT], F32, name="y_first")
+        y_last = sb.tile([P, 2, 2, G, NT], F32, name="y_last")
         y_codes = sb.tile([P, CHUNKS * G * NT], U32, name="y_codes", align_bytes=64)
         y_scales = sb.tile([P, CHUNKS * G * NT], U8, name="y_scales", align_bytes=64)
         for c in range(CHUNKS):
-            ys[c] = sb.tile([P, PACK, G, NT], F32, name="y%d" % c)
-            y_bf[c] = sb.tile([P, G * NT * PACK], BF16, name="y_bf%d" % c, align_bytes=64)
+            y_bf[c] = sb.tile([P, G * BANK], BF16, name="y_bf%d" % c, align_bytes=64)
 
-        def gate(c, g):
-            gates[c, g] = sb.tile([P, PACK * NT], F32, name="gate%d%d" % (c, g))
-            nc.scalar.activation(out=gates[c, g][:], in_=sums["w", c, g][:], func=SILU)
+        def gate(c, g, bank):
+            gates[c, g] = sb.tile([P, PACK, NT], F32, name="gate%d%d" % (c, g))
+            nc.scalar.activation(out=gates[c, g][:].rearrange("p z n -> p (z n)"), in_=banks[g][bank][:], func=SILU)
 
-        def multiply(c, g):
-            nc.vector.tensor_tensor(
-                out=ys[c][:, :, g, :],
-                in0=sums["u", c, g][:].rearrange("p (z n) -> p z n", z=PACK),
-                in1=gates[c, g][:].rearrange("p (z n) -> p z n", z=PACK),
-                op=MULT,
-            )
+        def multiply(out, c, g, bank, places):
+            sums = banks[g][bank][:].rearrange("p (z n) -> p z n", z=PACK)
+            nc.vector.tensor_tensor(out=out, in0=sums[:, places, :], in1=gates[c, g][:, places, :], op=MULT)
 
         queues = (nc.sync, nc.scalar)
-        y_out = out_0.rearrange("(g r) (c h n) -> c h r g n", g=G, c=CHUNKS, h=2)
+        halves = (slice(0, HALF), slice(HALF, P))
+        first_out = out_0.rearrange("(g r) (c h n) -> c h g r n", g=G, c=CHUNKS, h=2)[0]
+        last_out = out_0.rearrange("(g r e) (c h n) -> c h e r g n", g=G, e=2, c=CHUNKS, h=2)[1]
         words_out = out_1[0].rearrange("p n t -> p (n t)").bitcast(I32)
-        words_out = words_out.rearrange("(g p) (c h n) -> h (p c) g n", g=G, c=CHUNKS, h=2)
+        words_out = words_out.rearrange("(g p) (c h n) -> c h p g n", g=G, c=CHUNKS, h=2)
         scales_out = out_2[0].bitcast(I32).rearrange("(g b r) (c h n) -> h b (r c) g n", g=G, b=2, c=CHUNKS, h=2)
 
-        def store_y(c, h, lo, hi):
-            queues[h].dma_start(out=y_out[c][h][:, lo:hi, :], in_=ys[c][h * HALF : (h + 1) * HALF, :, lo:hi, :])
+        def store_first(g, h):
+            queues[h].dma_start(out=first_out[h][g], in_=y_first[halves[h], :, g, :])
 
-        def round_y(copy, c, g):
-            interleave(copy, y_bf[c][:, g * NT * PACK : (g + 1) * NT * PACK], ys[c][:, :, g, :], 0, NT)
+        def store_last(e, h):
+            queues[h].dma_start(out=last_out[h][e], in_=y_last[halves[h], e])
+
+        def round_first(copy, g):
+            interleave(copy, y_bf[0][:, g * BANK : (g + 1) * BANK], y_first[:, :, g, :], 0, NT)
+
+        def round_last(copy, g):
+            copy(
+                out=y_bf[1][:, g * BANK : (g + 1) * BANK].rearrange("p (c i a e) -> p c a e i", i=4, a=2, e=2),
+                in_=y_last[:, :, :, g, :].rearrange("p e a (c i) -> p c a e i", i=4),
+            )
 
         def quantize_y(c, lo, hi):
             cols = slice((c * G + lo) * NT, (c * G + hi) * NT)
             nc.vector.quantize_mx(
-                out=y_codes[:, cols].bitcast(FP8X4),
-                scales=y_scales[:, cols],
-                in_=y_bf[c][:, lo * NT * PACK : hi * NT * PACK],
+                out=y_codes[:, cols].bitcast(FP8X4), scales=y_scales[:, cols], in_=y_bf[c][:, lo * BANK : hi * BANK]
             )
 
-        def store_planes(h):
-            queues[h].dma_start(out=words_out[h], in_=y_codes[h * HALF : (h + 1) * HALF, :].bitcast(I32))
+        def store_words(c, h):
+            cols = slice(c * G * NT, (c + 1) * G * NT)
+            queues[h].dma_start(out=words_out[c][h], in_=y_codes[halves[h], cols].bitcast(I32))
+
+        def store_scales(h):
             for b in range(2):
                 first = h * HALF + 32 * b
                 queues[h].dma_start(out=scales_out[h][b], in_=y_scales[first : first + 4, :].bitcast(I32))
 
-        prep_weight("w")
         prep_x(0, X_SPLIT)
-        products("w", 0)
+        prep_weight("w")
+        products("w", 0, 0, range(PACK))
         prep_weight("u")
-        products("u", 0)
+        products("u", 0, 1, range(PACK))
         prep_x(1, CHUNK)
-        gate(0, 0)
-        gate(0, 1)
-        products("w", 1)
-        products("u", 1)
-        multiply(0, 0)
-        multiply(0, 1)
-        store_y(0, 0, 0, 1)
-        store_y(0, 1, 0, 1)
-        gate(1, 0)
-        store_y(0, 0, 1, 2)
-        store_y(0, 1, 1, 2)
-        gate(1, 1)
-        round_y(nc.vector.tensor_copy, 0, 0)
-        round_y(nc.scalar.copy, 0, 1)
-        multiply(1, 0)
-        multiply(1, 1)
-        round_y(nc.scalar.copy, 1, 0)
-        store_y(1, 0, 0, G)
-        store_y(1, 1, 0, G)
-        quantize_y(0, 0, 1)
-        round_y(nc.vector.tensor_copy, 1, 1)
-        quantize_y(0, 1, 2)
-        quantize_y(1, 0, G)
+        gate(0, 0, 0)
+        gate(0, 1, 0)
+        products("w", 1, 2, range(PACK))
+        products("u", 1, 3, (0, 2))
+        products("u", 1, 0, (1, 3))
+        for g in range(G):
+            multiply(y_first[:, :, g, :], 0, g, 1, slice(0, PACK))
+        for g in range(G):
+            store_first(g, 0)
+            store_first(g, 1)
+            gate(1, g, 2)
+        for g in range(G):
+            round_first(nc.vector.tensor_copy, g)
+        multiply(y_last[:, 0, :, 0, :], 1, 0, 3, slice(0, PACK, 2))
+        quantize_y(0, 0, G)
+        multiply(y_last[:, 0, :, 1, :], 1, 1, 3, slice(0, PACK, 2))
         for h in range(2):
-            store_planes(h)
+            store_words(0, h)
+            store_last(0, h)
+        for g in range(G):
+            multiply(y_last[:, 1, :, g, :], 1, g, 0, slice(1, PACK, 2))
+        round_last(nc.scalar.copy, 0)
+        for h in range(2):
+            store_last(1, h)
+        round_last(nc.vector.tensor_copy, 1)
+        for g in range(G):
+            quantize_y(1, g, g + 1)
+        for h in range(2):
+            store_words(1, h)
+            store_scales(h)

@@ -24,6 +24,7 @@ CHUNKS = N // CHUNK
 BANK = PACK * NT
 PADDED = HALF + PACK * P
 X_SPLIT = 176
+LAST_SPLIT = 64
 
 
 def interleave(copy, dst, src, lo, hi):
@@ -122,7 +123,7 @@ def tile_rows_pl_gswiglu_kernel(tc, x, w, u, out_0, out_1, out_2):
 
         def gate(c, g, bank):
             gates[c, g] = sb.tile([P, PACK, NT], F32, name="gate%d%d" % (c, g))
-            nc.scalar.activation(out=gates[c, g][:].rearrange("p z n -> p (z n)"), in_=banks[g][bank][:], func=SILU)
+            nc.scalar.activation(out=gates[c, g][:].rearrange("p z n -> p (z n)"), in_=banks[g][bank][:], func=SILU, bias=warm2[:, 0:1])
 
         def multiply(out, c, g, bank, places):
             sums = banks[g][bank][:].rearrange("p (z n) -> p z n", z=PACK)
@@ -145,10 +146,11 @@ def tile_rows_pl_gswiglu_kernel(tc, x, w, u, out_0, out_1, out_2):
         def round_first(copy, g):
             interleave(copy, y_bf[0][:, g * BANK : (g + 1) * BANK], y_first[:, :, g, :], 0, NT)
 
-        def round_last(copy, g):
+        def round_last(copy, g, lo, hi):
+            words = slice(g * BANK + lo * PACK, g * BANK + hi * PACK)
             copy(
-                out=y_bf[1][:, g * BANK : (g + 1) * BANK].rearrange("p (c i a e) -> p c a e i", i=4, a=2, e=2),
-                in_=y_last[:, :, :, g, :].rearrange("p e a (c i) -> p c a e i", i=4),
+                out=y_bf[1][:, words].rearrange("p (c i a e) -> p c a e i", i=4, a=2, e=2),
+                in_=y_last[:, :, :, g, lo:hi].rearrange("p e a (c i) -> p c a e i", i=4),
             )
 
         def quantize_y(c, lo, hi):
@@ -157,9 +159,9 @@ def tile_rows_pl_gswiglu_kernel(tc, x, w, u, out_0, out_1, out_2):
                 out=y_codes[:, cols].bitcast(FP8X4), scales=y_scales[:, cols], in_=y_bf[c][:, lo * BANK : hi * BANK]
             )
 
-        def store_words(c, h):
+        def store_words(queue, c, h):
             cols = slice(c * G * NT, (c + 1) * G * NT)
-            queues[h].dma_start(out=words_out[c][h], in_=y_codes[halves[h], cols].bitcast(I32))
+            queue.dma_start(out=words_out[c][h], in_=y_codes[halves[h], cols].bitcast(I32))
 
         def store_scales(h):
             for b in range(2):
@@ -185,20 +187,22 @@ def tile_rows_pl_gswiglu_kernel(tc, x, w, u, out_0, out_1, out_2):
             gate(1, g, 2)
         for g in range(G):
             round_first(nc.vector.tensor_copy, g)
-        multiply(y_last[:, 0, :, 0, :], 1, 0, 3, slice(0, PACK, 2))
         quantize_y(0, 0, G)
-        multiply(y_last[:, 0, :, 1, :], 1, 1, 3, slice(0, PACK, 2))
         for h in range(2):
-            store_words(0, h)
+            store_words(nc.sync, 0, h)
+        for g in range(G):
+            multiply(y_last[:, 0, :, g, :], 1, g, 3, slice(0, PACK, 2))
+        for h in range(2):
             store_last(0, h)
         for g in range(G):
             multiply(y_last[:, 1, :, g, :], 1, g, 0, slice(1, PACK, 2))
-        round_last(nc.scalar.copy, 0)
+        round_last(nc.scalar.copy, 0, 0, LAST_SPLIT)
         for h in range(2):
             store_last(1, h)
-        round_last(nc.vector.tensor_copy, 1)
+        round_last(nc.vector.tensor_copy, 0, LAST_SPLIT, NT)
+        round_last(nc.vector.tensor_copy, 1, 0, NT)
         for g in range(G):
             quantize_y(1, g, g + 1)
         for h in range(2):
-            store_words(1, h)
+            store_words(queues[h], 1, h)
             store_scales(h)

@@ -24,7 +24,6 @@ CHUNKS = N // CHUNK
 BANK = PACK * NT
 PADDED = HALF + PACK * P
 X_SPLIT = 176
-LAST_SPLIT = 64
 
 
 def interleave(copy, dst, src, lo, hi):
@@ -57,10 +56,10 @@ def tile_rows_pl_gswiglu_kernel(tc, x, w, u, out_0, out_1, out_2):
         load_weight("u", u)
         load_x(1)
 
-        warm = sb.tile([P, 8], F32, name="warm")
-        warm2 = sb.tile([P, 8], F32, name="warm2")
-        nc.vector.memset(warm[:], 0.0)
-        nc.scalar.activation(out=warm2[:], in_=warm[:], func=SILU)
+        zero = sb.tile([P, 1], F32, name="zero")
+        gate_bias = sb.tile([P, 1], F32, name="gate_bias")
+        nc.vector.memset(zero[:], 0.0)
+        nc.scalar.activation(out=gate_bias[:], in_=zero[:], func=SILU)
 
         grouped, codes, scales = {}, {}, {}
         for name in ("w", "u"):
@@ -87,122 +86,122 @@ def tile_rows_pl_gswiglu_kernel(tc, x, w, u, out_0, out_1, out_2):
                     in_=grouped[name][:, z * M : (z + 1) * M],
                 )
 
-        def prep_x(c, share):
-            interleave(nc.vector.tensor_copy, grouped[c], raw[c], 0, share)
-            if share < CHUNK:
-                interleave(nc.scalar.copy, grouped[c], raw[c], share, CHUNK)
-            nc.vector.quantize_mx(out=codes[c][:].bitcast(FP8X4), scales=scales[c][:], in_=grouped[c][:])
+        def quantize_x(c, lo, hi):
+            nc.vector.quantize_mx(
+                out=codes[c][:, lo:hi].bitcast(FP8X4),
+                scales=scales[c][:, lo:hi],
+                in_=grouped[c][:, lo * PACK : hi * PACK],
+            )
 
-        banks = [[ps.tile([P, BANK], F32, name="bank%d%d" % (g, k)) for k in range(4)] for g in range(G)]
+        banks = {(name, c, g): ps.tile([P, BANK], F32, name="bank_%s%d%d" % (name, c, g))
+                 for name in ("w", "u") for c in range(CHUNKS) for g in range(G)}
 
-        def products(name, c, bank, places):
-            for z in places:
-                for h in range(2):
-                    first = P * z + HALF * (1 - h)
-                    wcols = slice(first, first + P)
-                    xcols = slice(h * NT, (h + 1) * NT)
-                    for g in range(G):
-                        rows = slice(g * ROWS, (g + 1) * ROWS)
-                        nc.tensor.matmul_mx(
-                            out=banks[g][bank][:, z * NT : (z + 1) * NT],
-                            lhsT=codes[name][rows, wcols].bitcast(FP8X4),
-                            lhsT_scale=scales[name][rows, wcols],
-                            rhs=codes[c][rows, xcols].bitcast(FP8X4),
-                            rhs_scale=scales[c][rows, xcols],
-                            start=(h == 0),
-                            stop=(h == 1),
-                        )
+        def products(name, c, order):
+            for k, (z, h) in enumerate(order):
+                first = P * z + HALF * (1 - h)
+                wcols = slice(first, first + P)
+                xcols = slice(h * NT, (h + 1) * NT)
+                for g in range(G):
+                    rows = slice(g * ROWS, (g + 1) * ROWS)
+                    nc.tensor.matmul_mx(
+                        out=banks[name, c, g][:, z * NT : (z + 1) * NT],
+                        lhsT=codes[name][rows, wcols].bitcast(FP8X4),
+                        lhsT_scale=scales[name][rows, wcols],
+                        rhs=codes[c][rows, xcols].bitcast(FP8X4),
+                        rhs_scale=scales[c][rows, xcols],
+                        start=(k == 0),
+                        stop=(k == len(order) - 1),
+                    )
 
-        gates, y_bf = {}, {}
-        y_first = sb.tile([P, PACK, G, NT], F32, name="y_first")
-        y_last = sb.tile([P, 2, 2, G, NT], F32, name="y_last")
+        by_place = [(z, h) for z in range(PACK) for h in range(2)]
+        by_half = [(z, h) for h in range(2) for z in range(PACK)]
+
+        gates = {}
+        y_first = [sb.tile([P, PACK, NT], F32, name="y_first%d" % g) for g in range(G)]
+        y_last = sb.tile([P, PACK, G, NT], F32, name="y_last")
+        y = {(0, 0): y_first[0][:], (0, 1): y_first[1][:], (1, 0): y_last[:, :, 0, :], (1, 1): y_last[:, :, 1, :]}
+        y_bf = sb.tile([P, CHUNKS * G * BANK], BF16, name="y_bf", align_bytes=64)
         y_codes = sb.tile([P, CHUNKS * G * NT], U32, name="y_codes", align_bytes=64)
         y_scales = sb.tile([P, CHUNKS * G * NT], U8, name="y_scales", align_bytes=64)
-        for c in range(CHUNKS):
-            y_bf[c] = sb.tile([P, G * BANK], BF16, name="y_bf%d" % c, align_bytes=64)
 
-        def gate(c, g, bank):
-            gates[c, g] = sb.tile([P, PACK, NT], F32, name="gate%d%d" % (c, g))
-            nc.scalar.activation(out=gates[c, g][:].rearrange("p z n -> p (z n)"), in_=banks[g][bank][:], func=SILU, bias=warm2[:, 0:1])
+        def gate(c, g):
+            gates[c, g] = sb.tile([P, BANK], F32, name="gate%d%d" % (c, g))
+            nc.scalar.activation(out=gates[c, g][:], in_=banks["w", c, g][:], func=SILU, bias=gate_bias[:])
 
-        def multiply(out, c, g, bank, places):
-            sums = banks[g][bank][:].rearrange("p (z n) -> p z n", z=PACK)
-            nc.vector.tensor_tensor(out=out, in0=sums[:, places, :], in1=gates[c, g][:, places, :], op=MULT)
+        def multiply(c, g):
+            nc.vector.tensor_tensor(
+                out=y[c, g],
+                in0=banks["u", c, g][:].rearrange("p (z n) -> p z n", z=PACK),
+                in1=gates[c, g][:].rearrange("p (z n) -> p z n", z=PACK),
+                op=MULT,
+            )
+
+        def round_y(copy, c, g, lo=0, hi=NT):
+            unit = c * G + g
+            interleave(copy, y_bf[:, unit * BANK : (unit + 1) * BANK], y[c, g], lo, hi)
+
+        def quantize_y(first, last):
+            cols = slice(first * NT, last * NT)
+            nc.vector.quantize_mx(
+                out=y_codes[:, cols].bitcast(FP8X4), scales=y_scales[:, cols], in_=y_bf[:, first * BANK : last * BANK]
+            )
 
         queues = (nc.sync, nc.scalar)
         halves = (slice(0, HALF), slice(HALF, P))
         first_out = out_0.rearrange("(g r) (c h n) -> c h g r n", g=G, c=CHUNKS, h=2)[0]
-        last_out = out_0.rearrange("(g r e) (c h n) -> c h e r g n", g=G, e=2, c=CHUNKS, h=2)[1]
+        last_out = out_0.rearrange("(g r) (c h n) -> c h r g n", g=G, c=CHUNKS, h=2)[1]
         words_out = out_1[0].rearrange("p n t -> p (n t)").bitcast(I32)
-        words_out = words_out.rearrange("(g p) (c h n) -> c h p g n", g=G, c=CHUNKS, h=2)
+        words_out = words_out.rearrange("(g p) (c h n) -> h (p c) g n", g=G, c=CHUNKS, h=2)
         scales_out = out_2[0].bitcast(I32).rearrange("(g b r) (c h n) -> h b (r c) g n", g=G, b=2, c=CHUNKS, h=2)
 
         def store_first(g, h):
-            queues[h].dma_start(out=first_out[h][g], in_=y_first[halves[h], :, g, :])
+            queues[h].dma_start(out=first_out[h][g], in_=y_first[g][halves[h]])
 
-        def store_last(e, h):
-            queues[h].dma_start(out=last_out[h][e], in_=y_last[halves[h], e])
+        def store_last(h):
+            queues[h].dma_start(out=last_out[h], in_=y_last[halves[h]])
 
-        def round_first(copy, g):
-            interleave(copy, y_bf[0][:, g * BANK : (g + 1) * BANK], y_first[:, :, g, :], 0, NT)
-
-        def round_last(copy, g, lo, hi):
-            words = slice(g * BANK + lo * PACK, g * BANK + hi * PACK)
-            copy(
-                out=y_bf[1][:, words].rearrange("p (c i a e) -> p c a e i", i=4, a=2, e=2),
-                in_=y_last[:, :, :, g, lo:hi].rearrange("p e a (c i) -> p c a e i", i=4),
-            )
-
-        def quantize_y(c, lo, hi):
-            cols = slice((c * G + lo) * NT, (c * G + hi) * NT)
-            nc.vector.quantize_mx(
-                out=y_codes[:, cols].bitcast(FP8X4), scales=y_scales[:, cols], in_=y_bf[c][:, lo * BANK : hi * BANK]
-            )
-
-        def store_words(queue, c, h):
-            cols = slice(c * G * NT, (c + 1) * G * NT)
-            queue.dma_start(out=words_out[c][h], in_=y_codes[halves[h], cols].bitcast(I32))
-
-        def store_scales(h):
+        def store_planes(h):
+            queues[h].dma_start(out=words_out[h], in_=y_codes[halves[h], :].bitcast(I32))
             for b in range(2):
                 first = h * HALF + 32 * b
                 queues[h].dma_start(out=scales_out[h][b], in_=y_scales[first : first + 4, :].bitcast(I32))
 
-        prep_x(0, X_SPLIT)
+        interleave(nc.vector.tensor_copy, grouped[0], raw[0], 0, X_SPLIT)
+        interleave(nc.scalar.copy, grouped[0], raw[0], X_SPLIT, CHUNK)
+        quantize_x(0, 0, CHUNK)
         prep_weight("w")
-        products("w", 0, 0, range(PACK))
+        products("w", 0, by_place)
         prep_weight("u")
-        products("u", 0, 1, range(PACK))
-        prep_x(1, CHUNK)
-        gate(0, 0, 0)
-        gate(0, 1, 0)
-        products("w", 1, 2, range(PACK))
-        products("u", 1, 3, (0, 2))
-        products("u", 1, 0, (1, 3))
-        for g in range(G):
-            multiply(y_first[:, :, g, :], 0, g, 1, slice(0, PACK))
-        for g in range(G):
-            store_first(g, 0)
-            store_first(g, 1)
-            gate(1, g, 2)
-        for g in range(G):
-            round_first(nc.vector.tensor_copy, g)
-        quantize_y(0, 0, G)
-        for h in range(2):
-            store_words(nc.sync, 0, h)
-        for g in range(G):
-            multiply(y_last[:, 0, :, g, :], 1, g, 3, slice(0, PACK, 2))
-        for h in range(2):
-            store_last(0, h)
-        for g in range(G):
-            multiply(y_last[:, 1, :, g, :], 1, g, 0, slice(1, PACK, 2))
-        round_last(nc.scalar.copy, 0, 0, LAST_SPLIT)
-        for h in range(2):
-            store_last(1, h)
-        round_last(nc.vector.tensor_copy, 0, LAST_SPLIT, NT)
-        round_last(nc.vector.tensor_copy, 1, 0, NT)
-        for g in range(G):
-            quantize_y(1, g, g + 1)
-        for h in range(2):
-            store_words(queues[h], 1, h)
-            store_scales(h)
+        products("u", 0, by_place)
+        gate(0, 0)
+
+        interleave(nc.vector.tensor_copy, grouped[1], raw[1], 0, NT)
+        interleave(nc.vector.tensor_copy, grouped[1], raw[1], NT, X_SPLIT)
+        interleave(nc.scalar.copy, grouped[1], raw[1], X_SPLIT, CHUNK)
+        quantize_x(1, 0, NT)
+        quantize_x(1, NT, CHUNK)
+        gate(0, 1)
+        products("w", 1, by_half)
+        products("u", 1, by_half)
+
+        multiply(0, 0)
+        store_first(0, 0)
+        store_first(0, 1)
+        gate(1, 0)
+        multiply(0, 1)
+        store_first(1, 0)
+        store_first(1, 1)
+        gate(1, 1)
+        round_y(nc.vector.tensor_copy, 0, 0)
+        round_y(nc.vector.tensor_copy, 0, 1)
+        multiply(1, 0)
+        round_y(nc.scalar.copy, 1, 0)
+        multiply(1, 1)
+        store_last(0)
+        store_last(1)
+        quantize_y(0, 2)
+        round_y(nc.vector.tensor_copy, 1, 1)
+        quantize_y(2, 3)
+        quantize_y(3, 4)
+        store_planes(0)
+        store_planes(1)

@@ -24,6 +24,7 @@ CHUNKS = N // CHUNK
 BANK = PACK * NT
 PADDED = HALF + PACK * P
 X_SPLIT = 176
+LAST_X_SPLIT = 160
 
 
 def interleave(copy, dst, src, lo, hi):
@@ -117,9 +118,7 @@ def tile_rows_pl_gswiglu_kernel(tc, x, w, u, out_0, out_1, out_2):
         by_half = [(z, h) for h in range(2) for z in range(PACK)]
 
         gates = {}
-        y_first = [sb.tile([P, PACK, NT], F32, name="y_first%d" % g) for g in range(G)]
-        y_last = sb.tile([P, PACK, G, NT], F32, name="y_last")
-        y = {(0, 0): y_first[0][:], (0, 1): y_first[1][:], (1, 0): y_last[:, :, 0, :], (1, 1): y_last[:, :, 1, :]}
+        y = {(c, g): sb.tile([P, PACK, NT], F32, name="y%d%d" % (c, g)) for c in range(CHUNKS) for g in range(G)}
         y_bf = sb.tile([P, CHUNKS * G * BANK], BF16, name="y_bf", align_bytes=64)
         y_codes = sb.tile([P, CHUNKS * G * NT], U32, name="y_codes", align_bytes=64)
         y_scales = sb.tile([P, CHUNKS * G * NT], U8, name="y_scales", align_bytes=64)
@@ -130,7 +129,7 @@ def tile_rows_pl_gswiglu_kernel(tc, x, w, u, out_0, out_1, out_2):
 
         def multiply(c, g):
             nc.vector.tensor_tensor(
-                out=y[c, g],
+                out=y[c, g][:],
                 in0=banks["u", c, g][:].rearrange("p (z n) -> p z n", z=PACK),
                 in1=gates[c, g][:].rearrange("p (z n) -> p z n", z=PACK),
                 op=MULT,
@@ -148,20 +147,20 @@ def tile_rows_pl_gswiglu_kernel(tc, x, w, u, out_0, out_1, out_2):
 
         queues = (nc.sync, nc.scalar)
         halves = (slice(0, HALF), slice(HALF, P))
-        first_out = out_0.rearrange("(g r) (c h n) -> c h g r n", g=G, c=CHUNKS, h=2)[0]
-        last_out = out_0.rearrange("(g r) (c h n) -> c h r g n", g=G, c=CHUNKS, h=2)[1]
+        y_out = out_0.rearrange("(g r) (c h n) -> c g h r n", g=G, c=CHUNKS, h=2)
         words_out = out_1[0].rearrange("p n t -> p (n t)").bitcast(I32)
-        words_out = words_out.rearrange("(g p) (c h n) -> h (p c) g n", g=G, c=CHUNKS, h=2)
+        words_out = words_out.rearrange("(g p) (c h n) -> c h p g n", g=G, c=CHUNKS, h=2)
         scales_out = out_2[0].bitcast(I32).rearrange("(g b r) (c h n) -> h b (r c) g n", g=G, b=2, c=CHUNKS, h=2)
 
-        def store_first(g, h):
-            queues[h].dma_start(out=first_out[h][g], in_=y_first[g][halves[h]])
+        def store_y(c, g):
+            for h in range(2):
+                queues[h].dma_start(out=y_out[c][g][h], in_=y[c, g][halves[h]])
 
-        def store_last(h):
-            queues[h].dma_start(out=last_out[h], in_=y_last[halves[h]])
+        def store_words(c, h):
+            cols = slice(c * G * NT, (c + 1) * G * NT)
+            queues[h].dma_start(out=words_out[c][h], in_=y_codes[halves[h], cols].bitcast(I32))
 
-        def store_planes(h):
-            queues[h].dma_start(out=words_out[h], in_=y_codes[halves[h], :].bitcast(I32))
+        def store_scales(h):
             for b in range(2):
                 first = h * HALF + 32 * b
                 queues[h].dma_start(out=scales_out[h][b], in_=y_scales[first : first + 4, :].bitcast(I32))
@@ -174,34 +173,34 @@ def tile_rows_pl_gswiglu_kernel(tc, x, w, u, out_0, out_1, out_2):
         prep_weight("u")
         products("u", 0, by_place)
         gate(0, 0)
-
-        interleave(nc.vector.tensor_copy, grouped[1], raw[1], 0, NT)
-        interleave(nc.vector.tensor_copy, grouped[1], raw[1], NT, X_SPLIT)
-        interleave(nc.scalar.copy, grouped[1], raw[1], X_SPLIT, CHUNK)
-        quantize_x(1, 0, NT)
-        quantize_x(1, NT, CHUNK)
         gate(0, 1)
-        products("w", 1, by_half)
-        products("u", 1, by_half)
 
         multiply(0, 0)
-        store_first(0, 0)
-        store_first(0, 1)
-        gate(1, 0)
+        interleave(nc.vector.tensor_copy, grouped[1], raw[1], 0, NT)
+        interleave(nc.vector.tensor_copy, grouped[1], raw[1], NT, LAST_X_SPLIT)
+        interleave(nc.scalar.copy, grouped[1], raw[1], LAST_X_SPLIT, CHUNK)
+        store_y(0, 0)
+        quantize_x(1, 0, NT)
+        quantize_x(1, NT, CHUNK)
+        products("w", 1, by_half)
+        products("u", 1, by_half)
         multiply(0, 1)
-        store_first(1, 0)
-        store_first(1, 1)
+        store_y(0, 1)
+        gate(1, 0)
         gate(1, 1)
         round_y(nc.vector.tensor_copy, 0, 0)
         round_y(nc.vector.tensor_copy, 0, 1)
+        quantize_y(0, 2)
+        store_words(0, 0)
+        store_words(0, 1)
         multiply(1, 0)
+        store_y(1, 0)
         round_y(nc.scalar.copy, 1, 0)
         multiply(1, 1)
-        store_last(0)
-        store_last(1)
-        quantize_y(0, 2)
+        store_y(1, 1)
         round_y(nc.vector.tensor_copy, 1, 1)
         quantize_y(2, 3)
         quantize_y(3, 4)
-        store_planes(0)
-        store_planes(1)
+        for h in range(2):
+            store_words(1, h)
+            store_scales(h)

@@ -24,7 +24,7 @@ CHUNKS = N // CHUNK
 BANK = PACK * NT
 PADDED = HALF + PACK * P
 X_SPLIT = 176
-LAST_X_SPLIT = 160
+LAST_X_SPLIT = 192
 
 
 def interleave(copy, dst, src, lo, hi):
@@ -149,16 +149,15 @@ def tile_rows_pl_gswiglu_kernel(tc, x, w, u, out_0, out_1, out_2):
         halves = (slice(0, HALF), slice(HALF, P))
         y_out = out_0.rearrange("(g r) (c h n) -> c g h r n", g=G, c=CHUNKS, h=2)
         words_out = out_1[0].rearrange("p n t -> p (n t)").bitcast(I32)
-        words_out = words_out.rearrange("(g p) (c h n) -> c h p g n", g=G, c=CHUNKS, h=2)
+        words_out = words_out.rearrange("(g p) (c h n) -> h (p c) g n", g=G, c=CHUNKS, h=2)
         scales_out = out_2[0].bitcast(I32).rearrange("(g b r) (c h n) -> h b (r c) g n", g=G, b=2, c=CHUNKS, h=2)
 
         def store_y(c, g):
             for h in range(2):
                 queues[h].dma_start(out=y_out[c][g][h], in_=y[c, g][halves[h]])
 
-        def store_words(c, h):
-            cols = slice(c * G * NT, (c + 1) * G * NT)
-            queues[h].dma_start(out=words_out[c][h], in_=y_codes[halves[h], cols].bitcast(I32))
+        def store_words(h):
+            queues[h].dma_start(out=words_out[h], in_=y_codes[halves[h], :].bitcast(I32))
 
         def store_scales(h):
             for b in range(2):
@@ -173,34 +172,30 @@ def tile_rows_pl_gswiglu_kernel(tc, x, w, u, out_0, out_1, out_2):
         prep_weight("u")
         products("u", 0, by_place)
         gate(0, 0)
-        gate(0, 1)
 
-        multiply(0, 0)
         interleave(nc.vector.tensor_copy, grouped[1], raw[1], 0, NT)
         interleave(nc.vector.tensor_copy, grouped[1], raw[1], NT, LAST_X_SPLIT)
         interleave(nc.scalar.copy, grouped[1], raw[1], LAST_X_SPLIT, CHUNK)
-        store_y(0, 0)
         quantize_x(1, 0, NT)
         quantize_x(1, NT, CHUNK)
+        gate(0, 1)
         products("w", 1, by_half)
         products("u", 1, by_half)
-        multiply(0, 1)
-        store_y(0, 1)
-        gate(1, 0)
-        gate(1, 1)
-        round_y(nc.vector.tensor_copy, 0, 0)
-        round_y(nc.vector.tensor_copy, 0, 1)
-        quantize_y(0, 2)
-        store_words(0, 0)
-        store_words(0, 1)
+        for g in range(G):
+            multiply(0, g)
+            store_y(0, g)
+            gate(1, g)
+        for g in range(G):
+            round_y(nc.vector.tensor_copy, 0, g)
         multiply(1, 0)
         store_y(1, 0)
         round_y(nc.scalar.copy, 1, 0)
         multiply(1, 1)
         store_y(1, 1)
+        quantize_y(0, 2)
         round_y(nc.vector.tensor_copy, 1, 1)
         quantize_y(2, 3)
         quantize_y(3, 4)
         for h in range(2):
-            store_words(1, h)
+            store_words(h)
             store_scales(h)

@@ -24,7 +24,6 @@ CHUNKS = N // CHUNK
 BANK = PACK * NT
 PADDED = HALF + PACK * P
 X_SPLIT = 176
-LAST_X_SPLIT = 192
 
 
 def interleave(copy, dst, src, lo, hi):
@@ -174,8 +173,7 @@ def tile_rows_pl_gswiglu_kernel(tc, x, w, u, out_0, out_1, out_2):
         gate(0, 0)
 
         interleave(nc.vector.tensor_copy, grouped[1], raw[1], 0, NT)
-        interleave(nc.vector.tensor_copy, grouped[1], raw[1], NT, LAST_X_SPLIT)
-        interleave(nc.scalar.copy, grouped[1], raw[1], LAST_X_SPLIT, CHUNK)
+        interleave(nc.vector.tensor_copy, grouped[1], raw[1], NT, CHUNK)
         quantize_x(1, 0, NT)
         quantize_x(1, NT, CHUNK)
         gate(0, 1)

@@ -24,6 +24,7 @@ CHUNKS = N // CHUNK
 BANK = PACK * NT
 PADDED = HALF + PACK * P
 X_SPLIT = 176
+WARM_UPS = 3
 
 
 def interleave(copy, dst, src, lo, hi):
@@ -166,6 +167,18 @@ def tile_rows_pl_gswiglu_kernel(tc, x, w, u, out_0, out_1, out_2):
         interleave(nc.vector.tensor_copy, grouped[0], raw[0], 0, X_SPLIT)
         interleave(nc.scalar.copy, grouped[0], raw[0], X_SPLIT, CHUNK)
         quantize_x(0, 0, CHUNK)
+        for repeat in range(WARM_UPS):
+            for g in range(G):
+                rows = slice(g * ROWS, (g + 1) * ROWS)
+                nc.tensor.matmul_mx(
+                    out=banks["w", 1, g][:, 0:NT],
+                    lhsT=codes[0][rows, 0:P].bitcast(FP8X4),
+                    lhsT_scale=scales[0][rows, 0:P],
+                    rhs=codes[0][rows, 0:NT].bitcast(FP8X4),
+                    rhs_scale=scales[0][rows, 0:NT],
+                    start=True,
+                    stop=True,
+                )
         prep_weight("w")
         products("w", 0, by_place)
         prep_weight("u")

@@ -96,22 +96,30 @@ def tile_rows_pl_gswiglu_kernel(tc, x, w, u, out_0, out_1, out_2):
 
         banks = {(name, c, g): ps.tile([P, BANK], F32, name="bank_%s%d%d" % (name, c, g))
                  for name in ("w", "u") for c in range(CHUNKS) for g in range(G)}
+        first_low = banks["u", 1, 0]
+        banks["u", 1, 0] = banks["w", 0, 0]
 
-        def products(name, c, order):
+        def products(name, c, order, low_bank=None):
             for k, (z, h) in enumerate(order):
                 first = P * z + HALF * (1 - h)
                 wcols = slice(first, first + P)
                 xcols = slice(h * NT, (h + 1) * NT)
                 for g in range(G):
                     rows = slice(g * ROWS, (g + 1) * ROWS)
+                    bank, opens, closes = banks[name, c, g], 0, len(order) - 1
+                    if low_bank is not None and g == 0:
+                        if z < 2:
+                            bank, closes = low_bank, len(order) // 2 - 1
+                        else:
+                            opens = len(order) // 2
                     nc.tensor.matmul_mx(
-                        out=banks[name, c, g][:, z * NT : (z + 1) * NT],
+                        out=bank[:, z * NT : (z + 1) * NT],
                         lhsT=codes[name][rows, wcols].bitcast(FP8X4),
                         lhsT_scale=scales[name][rows, wcols],
                         rhs=codes[c][rows, xcols].bitcast(FP8X4),
                         rhs_scale=scales[c][rows, xcols],
-                        start=(k == 0),
-                        stop=(k == len(order) - 1),
+                        start=(k == opens),
+                        stop=(k == closes),
                     )
 
         by_place = [(z, h) for z in range(PACK) for h in range(2)]
@@ -127,11 +135,11 @@ def tile_rows_pl_gswiglu_kernel(tc, x, w, u, out_0, out_1, out_2):
             gates[c, g] = sb.tile([P, BANK], F32, name="gate%d%d" % (c, g))
             nc.scalar.activation(out=gates[c, g][:], in_=banks["w", c, g][:], func=SILU, bias=gate_bias[:])
 
-        def multiply(c, g):
+        def multiply(c, g, bank, places):
             nc.vector.tensor_tensor(
-                out=y[c, g][:],
-                in0=banks["u", c, g][:].rearrange("p (z n) -> p z n", z=PACK),
-                in1=gates[c, g][:].rearrange("p (z n) -> p z n", z=PACK),
+                out=y[c, g][:, places, :],
+                in0=bank[:].rearrange("p (z n) -> p z n", z=PACK)[:, places, :],
+                in1=gates[c, g][:].rearrange("p (z n) -> p z n", z=PACK)[:, places, :],
                 op=MULT,
             )
 
@@ -182,7 +190,7 @@ def tile_rows_pl_gswiglu_kernel(tc, x, w, u, out_0, out_1, out_2):
         prep_weight("w")
         products("w", 0, by_place)
         prep_weight("u")
-        products("u", 0, by_place)
+        products("u", 0, by_place, first_low)
         gate(0, 0)
 
         interleave(nc.vector.tensor_copy, grouped[1], raw[1], 0, NT)
@@ -192,16 +200,20 @@ def tile_rows_pl_gswiglu_kernel(tc, x, w, u, out_0, out_1, out_2):
         gate(0, 1)
         products("w", 1, by_half)
         products("u", 1, by_half)
-        for g in range(G):
-            multiply(0, g)
-            store_y(0, g)
-            gate(1, g)
+        every = slice(0, PACK)
+        multiply(0, 0, first_low, slice(0, 2))
+        multiply(0, 0, banks["u", 0, 0], slice(2, PACK))
+        store_y(0, 0)
+        gate(1, 0)
+        multiply(0, 1, banks["u", 0, 1], every)
+        store_y(0, 1)
+        gate(1, 1)
         for g in range(G):
             round_y(nc.vector.tensor_copy, 0, g)
-        multiply(1, 0)
+        multiply(1, 0, banks["u", 1, 0], every)
         store_y(1, 0)
         round_y(nc.scalar.copy, 1, 0)
-        multiply(1, 1)
+        multiply(1, 1, banks["u", 1, 1], every)
         store_y(1, 1)
         quantize_y(0, 2)
         round_y(nc.vector.tensor_copy, 1, 1)

@@ -13,6 +13,7 @@ U8 = mybir.dt.uint8
 FP8X4 = mybir.dt.float8_e4m3fn_x4
 SILU = mybir.ActivationFunctionType.Silu
 MULT = mybir.AluOpType.mult
+ADD = mybir.AluOpType.add
 
 P = 128
 PACK = 4
@@ -143,6 +144,9 @@ def tile_rows_pl_gswiglu_kernel(tc, x, w, u, out_0, out_1, out_2):
                 op=MULT,
             )
 
+        def pool_copy(out, in_):
+            nc.gpsimd.tensor_scalar(out=out, in0=in_, scalar1=1.0, scalar2=-0.0, op0=MULT, op1=ADD)
+
         def round_y(copy, c, g, lo=0, hi=NT):
             unit = c * G + g
             interleave(copy, y_bf[:, unit * BANK : (unit + 1) * BANK], y[c, g], lo, hi)
@@ -208,8 +212,8 @@ def tile_rows_pl_gswiglu_kernel(tc, x, w, u, out_0, out_1, out_2):
         multiply(0, 1, banks["u", 0, 1], every)
         store_y(0, 1)
         gate(1, 1)
-        for g in range(G):
-            round_y(nc.vector.tensor_copy, 0, g)
+        round_y(nc.vector.tensor_copy, 0, 0)
+        round_y(pool_copy, 0, 1)
         multiply(1, 0, banks["u", 1, 0], every)
         store_y(1, 0)
         round_y(nc.scalar.copy, 1, 0)

@@ -159,14 +159,14 @@ def tile_rows_pl_gswiglu_kernel(tc, x, w, u, out_0, out_1, out_2):
 
         queues = (nc.sync, nc.scalar)
         halves = (slice(0, HALF), slice(HALF, P))
-        y_out = out_0.rearrange("(g r) (c h n) -> c g h r n", g=G, c=CHUNKS, h=2)
+        y_out = out_0.rearrange("(g q z) (c h n) -> c g h q z n", g=G, z=PACK, c=CHUNKS, h=2)
         words_out = out_1[0].rearrange("p n t -> p (n t)").bitcast(I32)
         words_out = words_out.rearrange("(g p) (c h n) -> h (p c) g n", g=G, c=CHUNKS, h=2)
         scales_out = out_2[0].bitcast(I32).rearrange("(g b r) (c h n) -> h b (r c) g n", g=G, b=2, c=CHUNKS, h=2)
 
-        def store_y(c, g):
+        def store_y(c, g, places=slice(0, PACK)):
             for h in range(2):
-                queues[h].dma_start(out=y_out[c][g][h], in_=y[c, g][halves[h]])
+                queues[h].dma_start(out=y_out[c][g][h][:, places, :], in_=y[c, g][halves[h], places, :])
 
         def store_words(h):
             queues[h].dma_start(out=words_out[h], in_=y_codes[halves[h], :].bitcast(I32))
@@ -206,8 +206,9 @@ def tile_rows_pl_gswiglu_kernel(tc, x, w, u, out_0, out_1, out_2):
         products("u", 1, by_half)
         every = slice(0, PACK)
         multiply(0, 0, first_low, slice(0, 2))
+        store_y(0, 0, slice(0, 2))
         multiply(0, 0, banks["u", 0, 0], slice(2, PACK))
-        store_y(0, 0)
+        store_y(0, 0, slice(2, PACK))
         gate(1, 0)
         multiply(0, 1, banks["u", 0, 1], every)
         store_y(0, 1)

@@ -95,54 +95,54 @@ def tile_rows_pl_gswiglu_kernel(tc, x, w, u, out_0, out_1, out_2):
                 in_=grouped[c][:, lo * PACK : hi * PACK],
             )
 
-        banks = {(name, c, g): ps.tile([P, BANK], F32, name="bank_%s%d%d" % (name, c, g))
-                 for name in ("w", "u") for c in range(CHUNKS) for g in range(G)}
-        first_low = banks["u", 1, 0]
-        banks["u", 1, 0] = banks["w", 0, 0]
+        banks = [[ps.tile([P, PACK, NT], F32, name="bank%d%d" % (g, i)) for i in range(4)] for g in range(G)]
+        home = {}
+        for pair in range(2):
+            home["w", 0, 0, pair] = banks[0][0]
+            home["u", 0, 0, pair] = banks[0][1 + pair]
+            home["w", 1, 0, pair] = banks[0][3 - 3 * pair]
+            home["u", 1, 0, pair] = banks[0][1 + pair]
+            for c in range(CHUNKS):
+                home["w", c, 1, pair] = banks[1][2 * c]
+                home["u", c, 1, pair] = banks[1][2 * c + 1]
+        split = {("u", 0, 0), ("w", 1, 0), ("u", 1, 0)}
 
-        def products(name, c, order, low_bank=None):
-            for k, (z, h) in enumerate(order):
+        def products(name, c, order):
+            for z, h in order:
                 first = P * z + HALF * (1 - h)
                 wcols = slice(first, first + P)
                 xcols = slice(h * NT, (h + 1) * NT)
                 for g in range(G):
                     rows = slice(g * ROWS, (g + 1) * ROWS)
-                    bank, opens, closes = banks[name, c, g], 0, len(order) - 1
-                    if low_bank is not None and g == 0:
-                        if z < 2:
-                            bank, closes = low_bank, len(order) // 2 - 1
-                        else:
-                            opens = len(order) // 2
+                    group = [e for e in order if e[0] // 2 == z // 2] if (name, c, g) in split else order
                     nc.tensor.matmul_mx(
-                        out=bank[:, z * NT : (z + 1) * NT],
+                        out=home[name, c, g, z // 2][:, z, :],
                         lhsT=codes[name][rows, wcols].bitcast(FP8X4),
                         lhsT_scale=scales[name][rows, wcols],
                         rhs=codes[c][rows, xcols].bitcast(FP8X4),
                         rhs_scale=scales[c][rows, xcols],
-                        start=(k == opens),
-                        stop=(k == closes),
+                        start=((z, h) == group[0]),
+                        stop=((z, h) == group[-1]),
                     )
 
         by_place = [(z, h) for z in range(PACK) for h in range(2)]
         by_half = [(z, h) for h in range(2) for z in range(PACK)]
+        every = slice(0, PACK)
+        pairs = (slice(0, 2), slice(2, PACK))
 
-        gates = {}
+        gates = {(c, g): sb.tile([P, PACK, NT], F32, name="gate%d%d" % (c, g)) for c in range(CHUNKS) for g in range(G)}
         y = {(c, g): sb.tile([P, PACK, NT], F32, name="y%d%d" % (c, g)) for c in range(CHUNKS) for g in range(G)}
         y_bf = sb.tile([P, CHUNKS * G * BANK], BF16, name="y_bf", align_bytes=64)
         y_codes = sb.tile([P, CHUNKS * G * NT], U32, name="y_codes", align_bytes=64)
         y_scales = sb.tile([P, CHUNKS * G * NT], U8, name="y_scales", align_bytes=64)
 
-        def gate(c, g):
-            gates[c, g] = sb.tile([P, BANK], F32, name="gate%d%d" % (c, g))
-            nc.scalar.activation(out=gates[c, g][:], in_=banks["w", c, g][:], func=SILU, bias=gate_bias[:])
+        def gate(c, g, places=every):
+            bank = home["w", c, g, places.start // 2]
+            nc.scalar.activation(out=gates[c, g][:, places, :], in_=bank[:, places, :], func=SILU, bias=gate_bias[:])
 
-        def multiply(c, g, bank, places):
-            nc.vector.tensor_tensor(
-                out=y[c, g][:, places, :],
-                in0=bank[:].rearrange("p (z n) -> p z n", z=PACK)[:, places, :],
-                in1=gates[c, g][:].rearrange("p (z n) -> p z n", z=PACK)[:, places, :],
-                op=MULT,
-            )
+        def multiply(c, g, places=every):
+            bank = home["u", c, g, places.start // 2]
+            nc.vector.tensor_tensor(out=y[c, g][:, places, :], in0=bank[:, places, :], in1=gates[c, g][:, places, :], op=MULT)
 
         def pool_copy(out, in_):
             nc.gpsimd.tensor_scalar(out=out, in0=in_, scalar1=1.0, scalar2=-0.0, op0=MULT, op1=ADD)
@@ -164,7 +164,7 @@ def tile_rows_pl_gswiglu_kernel(tc, x, w, u, out_0, out_1, out_2):
         words_out = words_out.rearrange("(g p) (c h n) -> h (p c) g n", g=G, c=CHUNKS, h=2)
         scales_out = out_2[0].bitcast(I32).rearrange("(g b r) (c h n) -> h b (r c) g n", g=G, b=2, c=CHUNKS, h=2)
 
-        def store_y(c, g, places=slice(0, PACK)):
+        def store_y(c, g, places=every):
             for h in range(2):
                 queues[h].dma_start(out=y_out[c][g][h][:, places, :], in_=y[c, g][halves[h], places, :])
 
@@ -183,7 +183,7 @@ def tile_rows_pl_gswiglu_kernel(tc, x, w, u, out_0, out_1, out_2):
             for g in range(G):
                 rows = slice(g * ROWS, (g + 1) * ROWS)
                 nc.tensor.matmul_mx(
-                    out=banks["w", 1, g][:, 0:NT],
+                    out=home["w", 1, g, 0][:, 0, :],
                     lhsT=codes[0][rows, 0:P].bitcast(FP8X4),
                     lhsT_scale=scales[0][rows, 0:P],
                     rhs=codes[0][rows, 0:NT].bitcast(FP8X4),
@@ -194,7 +194,7 @@ def tile_rows_pl_gswiglu_kernel(tc, x, w, u, out_0, out_1, out_2):
         prep_weight("w")
         products("w", 0, by_place)
         prep_weight("u")
-        products("u", 0, by_place, first_low)
+        products("u", 0, by_place)
         gate(0, 0)
 
         interleave(nc.vector.tensor_copy, grouped[1], raw[1], 0, NT)
@@ -203,22 +203,24 @@ def tile_rows_pl_gswiglu_kernel(tc, x, w, u, out_0, out_1, out_2):
         quantize_x(1, NT, CHUNK)
         gate(0, 1)
         products("w", 1, by_half)
-        products("u", 1, by_half)
-        every = slice(0, PACK)
-        multiply(0, 0, first_low, slice(0, 2))
-        store_y(0, 0, slice(0, 2))
-        multiply(0, 0, banks["u", 0, 0], slice(2, PACK))
-        store_y(0, 0, slice(2, PACK))
-        gate(1, 0)
-        multiply(0, 1, banks["u", 0, 1], every)
+        for pair in pairs:
+            multiply(0, 0, pair)
+            store_y(0, 0, pair)
+        products("u", 1, by_place)
+        for pair in pairs:
+            gate(1, 0, pair)
+        multiply(0, 1)
         store_y(0, 1)
-        gate(1, 1)
+        for pair in pairs:
+            gate(1, 1, pair)
         round_y(nc.vector.tensor_copy, 0, 0)
         round_y(pool_copy, 0, 1)
-        multiply(1, 0, banks["u", 1, 0], every)
+        for pair in pairs:
+            multiply(1, 0, pair)
         store_y(1, 0)
         round_y(nc.scalar.copy, 1, 0)
-        multiply(1, 1, banks["u", 1, 1], every)
+        for pair in pairs:
+            multiply(1, 1, pair)
         store_y(1, 1)
         quantize_y(0, 2)
         round_y(nc.vector.tensor_copy, 1, 1)

@@ -25,6 +25,7 @@ CHUNKS = N // CHUNK
 BANK = PACK * NT
 PADDED = HALF + PACK * P
 X_SPLIT = 176
+POOL_FROM = 80
 WARM_UPS = 3
 
 
@@ -214,7 +215,8 @@ def tile_rows_pl_gswiglu_kernel(tc, x, w, u, out_0, out_1, out_2):
         for pair in pairs:
             gate(1, 1, pair)
         round_y(nc.vector.tensor_copy, 0, 0)
-        round_y(pool_copy, 0, 1)
+        round_y(nc.vector.tensor_copy, 0, 1, 0, POOL_FROM)
+        round_y(pool_copy, 0, 1, POOL_FROM, NT)
         for pair in pairs:
             multiply(1, 0, pair)
         store_y(1, 0)

@@ -175,7 +175,7 @@ def tile_rows_pl_gswiglu_kernel(tc, x, w, u, out_0, out_1, out_2):
         def store_scales(h):
             for b in range(2):
                 first = h * HALF + 32 * b
-                queues[h].dma_start(out=scales_out[h][b], in_=y_scales[first : first + 4, :].bitcast(I32))
+                nc.sync.dma_start(out=scales_out[h][b], in_=y_scales[first : first + 4, :].bitcast(I32))
 
         interleave(nc.vector.tensor_copy, grouped[0], raw[0], 0, X_SPLIT)
         interleave(nc.scalar.copy, grouped[0], raw[0], X_SPLIT, CHUNK)
@@ -230,4 +230,5 @@ def tile_rows_pl_gswiglu_kernel(tc, x, w, u, out_0, out_1, out_2):
         quantize_y(3, 4)
         for h in range(2):
             store_words(h)
+        for h in range(2):
             store_scales(h)

from contextlib import ExitStack

import concourse.mybir as mybir

G, D, M, N = 2, 256, 256, 512
FLOPS = 2 * 2 * G * D * M * N

F32 = mybir.dt.float32
BF16 = mybir.dt.bfloat16
I32 = mybir.dt.int32
U32 = mybir.dt.uint32
U8 = mybir.dt.uint8
FP8X4 = mybir.dt.float8_e4m3fn_x4
SILU = mybir.ActivationFunctionType.Silu
MULT = mybir.AluOpType.mult
ADD = mybir.AluOpType.add

P = 128
PACK = 4
ROWS = D // PACK
HALF = P // 2
NT = 128
CHUNK = 2 * NT
CHUNKS = N // CHUNK
BANK = PACK * NT
PADDED = HALF + PACK * P
X_SPLIT = 176
POOL_FROM = 80
WARM_UPS = 3


def interleave(copy, dst, src, lo, hi):
    copy(
        out=dst[:, lo * PACK : hi * PACK].rearrange("p (c i t) -> p c t i", i=4, t=PACK),
        in_=src[:, :, lo:hi].rearrange("p t (c i) -> p c t i", i=4),
    )


def tile_rows_pl_gswiglu_kernel(tc, x, w, u, out_0, out_1, out_2):
    nc = tc.nc
    with ExitStack() as ctx:
        sb = ctx.enter_context(tc.tile_pool(name="sb", bufs=1))
        ps = ctx.enter_context(tc.psum_pool(name="ps", bufs=1))
        ctx.enter_context(tc.manual_schedule())

        x_rows = x.rearrange("g (p j) n -> (g p) j n", j=PACK)
        raw = {}

        def load_weight(name, src):
            raw[name] = sb.tile([P, PACK, M], F32, name=name + "_raw")
            nc.sync.dma_start(out=raw[name][:], in_=src.rearrange("g (p j) m -> (g p) j m", j=PACK))

        def load_x(c):
            raw[c] = sb.tile([P, PACK, CHUNK], F32, name="x_raw%d" % c)
            nc.sync.dma_start(out=raw[c][:], in_=x_rows[:, :, c * CHUNK : (c + 1) * CHUNK])

        load_x(0)
        load_weight("w", w)
        load_weight("u", u)
        load_x(1)

        zero = sb.tile([P, 1], F32, name="zero")
        gate_bias = sb.tile([P, 1], F32, name="gate_bias")
        nc.vector.memset(zero[:], 0.0)
        nc.scalar.activation(out=gate_bias[:], in_=zero[:], func=SILU)

        grouped, codes, scales = {}, {}, {}
        for name in ("w", "u"):
            grouped[name] = sb.tile([P, PACK * M], BF16, name=name + "_bf", align_bytes=64)
            codes[name] = sb.tile([P, PADDED], U32, name=name + "_codes", align_bytes=64)
            scales[name] = sb.tile([P, PADDED], U8, name=name + "_scales", align_bytes=64)
            nc.vector.memset(codes[name][:], 0)
            nc.vector.memset(scales[name][:].bitcast(U32), 0)
        for c in range(CHUNKS):
            grouped[c] = sb.tile([P, CHUNK * PACK], BF16, name="x_bf%d" % c, align_bytes=64)
            codes[c] = sb.tile([P, CHUNK], U32, name="x_codes%d" % c, align_bytes=64)
            scales[c] = sb.tile([P, CHUNK], U8, name="x_scales%d" % c, align_bytes=64)

        def prep_weight(name):
            src = raw[name][:].rearrange("p j (q z) -> p q z j", z=PACK)
            dst = grouped[name][:].rearrange("p (z q j) -> p q z j", z=PACK, j=PACK)
            nc.vector.tensor_copy(out=dst[:, :, 0:2, :], in_=src[:, :, 0:2, :])
            nc.scalar.copy(out=dst[:, :, 2:PACK, :], in_=src[:, :, 2:PACK, :])
            for z in range(PACK):
                win = slice(HALF + P * z, P + P * z)
                nc.vector.quantize_mx(
                    out=codes[name][:, win].bitcast(FP8X4),
                    scales=scales[name][:, win],
                    in_=grouped[name][:, z * M : (z + 1) * M],
                )

        def quantize_x(c, lo, hi):
            nc.vector.quantize_mx(
                out=codes[c][:, lo:hi].bitcast(FP8X4),
                scales=scales[c][:, lo:hi],
                in_=grouped[c][:, lo * PACK : hi * PACK],
            )

        banks = [[ps.tile([P, PACK, NT], F32, name="bank%d%d" % (g, i)) for i in range(4)] for g in range(G)]
        home = {}
        for pair in range(2):
            home["w", 0, 0, pair] = banks[0][0]
            home["u", 0, 0, pair] = banks[0][1 + pair]
            home["w", 1, 0, pair] = banks[0][3 - 3 * pair]
            home["u", 1, 0, pair] = banks[0][1 + pair]
            for c in range(CHUNKS):
                home["w", c, 1, pair] = banks[1][2 * c]
                home["u", c, 1, pair] = banks[1][2 * c + 1]
        split = {("u", 0, 0), ("w", 1, 0), ("u", 1, 0)}

        def products(name, c, order):
            for z, h in order:
                first = P * z + HALF * (1 - h)
                wcols = slice(first, first + P)
                xcols = slice(h * NT, (h + 1) * NT)
                for g in range(G):
                    rows = slice(g * ROWS, (g + 1) * ROWS)
                    group = [e for e in order if e[0] // 2 == z // 2] if (name, c, g) in split else order
                    nc.tensor.matmul_mx(
                        out=home[name, c, g, z // 2][:, z, :],
                        lhsT=codes[name][rows, wcols].bitcast(FP8X4),
                        lhsT_scale=scales[name][rows, wcols],
                        rhs=codes[c][rows, xcols].bitcast(FP8X4),
                        rhs_scale=scales[c][rows, xcols],
                        start=((z, h) == group[0]),
                        stop=((z, h) == group[-1]),
                    )

        by_place = [(z, h) for z in range(PACK) for h in range(2)]
        by_half = [(z, h) for h in range(2) for z in range(PACK)]
        every = slice(0, PACK)
        pairs = (slice(0, 2), slice(2, PACK))

        gates = {(c, g): sb.tile([P, PACK, NT], F32, name="gate%d%d" % (c, g)) for c in range(CHUNKS) for g in range(G)}
        y = {(c, g): sb.tile([P, PACK, NT], F32, name="y%d%d" % (c, g)) for c in range(CHUNKS) for g in range(G)}
        y_bf = sb.tile([P, CHUNKS * G * BANK], BF16, name="y_bf", align_bytes=64)
        y_codes = sb.tile([P, CHUNKS * G * NT], U32, name="y_codes", align_bytes=64)
        y_scales = sb.tile([P, CHUNKS * G * NT], U8, name="y_scales", align_bytes=64)

        def gate(c, g, places=every):
            bank = home["w", c, g, places.start // 2]
            nc.scalar.activation(out=gates[c, g][:, places, :], in_=bank[:, places, :], func=SILU, bias=gate_bias[:])

        def multiply(c, g, places=every):
            bank = home["u", c, g, places.start // 2]
            nc.vector.tensor_tensor(out=y[c, g][:, places, :], in0=bank[:, places, :], in1=gates[c, g][:, places, :], op=MULT)

        def pool_copy(out, in_):
            nc.gpsimd.tensor_scalar(out=out, in0=in_, scalar1=1.0, scalar2=-0.0, op0=MULT, op1=ADD)

        def round_y(copy, c, g, lo=0, hi=NT):
            unit = c * G + g
            interleave(copy, y_bf[:, unit * BANK : (unit + 1) * BANK], y[c, g], lo, hi)

        def quantize_y(first, last):
            cols = slice(first * NT, last * NT)
            nc.vector.quantize_mx(
                out=y_codes[:, cols].bitcast(FP8X4), scales=y_scales[:, cols], in_=y_bf[:, first * BANK : last * BANK]
            )

        queues = (nc.sync, nc.scalar)
        halves = (slice(0, HALF), slice(HALF, P))
        y_out = out_0.rearrange("(g q z) (c h n) -> c g h q z n", g=G, z=PACK, c=CHUNKS, h=2)
        words_out = out_1[0].rearrange("p n t -> p (n t)").bitcast(I32)
        words_out = words_out.rearrange("(g p) (c h n) -> h (p c) g n", g=G, c=CHUNKS, h=2)
        scales_out = out_2[0].bitcast(I32).rearrange("(g b r) (c h n) -> h b (r c) g n", g=G, b=2, c=CHUNKS, h=2)

        def store_y(c, g, places=every):
            for h in range(2):
                queues[h].dma_start(out=y_out[c][g][h][:, places, :], in_=y[c, g][halves[h], places, :])

        def store_words(h):
            queues[h].dma_start(out=words_out[h], in_=y_codes[halves[h], :].bitcast(I32))

        def store_scales(h):
            for b in range(2):
                first = h * HALF + 32 * b
                nc.sync.dma_start(out=scales_out[h][b], in_=y_scales[first : first + 4, :].bitcast(I32))

        interleave(nc.vector.tensor_copy, grouped[0], raw[0], 0, X_SPLIT)
        interleave(nc.scalar.copy, grouped[0], raw[0], X_SPLIT, CHUNK)
        quantize_x(0, 0, CHUNK)
        for repeat in range(WARM_UPS):
            for g in range(G):
                rows = slice(g * ROWS, (g + 1) * ROWS)
                nc.tensor.matmul_mx(
                    out=home["w", 1, g, 0][:, 0, :],
                    lhsT=codes[0][rows, 0:P].bitcast(FP8X4),
                    lhsT_scale=scales[0][rows, 0:P],
                    rhs=codes[0][rows, 0:NT].bitcast(FP8X4),
                    rhs_scale=scales[0][rows, 0:NT],
                    start=True,
                    stop=True,
                )
        prep_weight("w")
        products("w", 0, by_place)
        prep_weight("u")
        products("u", 0, by_place)
        gate(0, 0)

        interleave(nc.vector.tensor_copy, grouped[1], raw[1], 0, NT)
        interleave(nc.vector.tensor_copy, grouped[1], raw[1], NT, CHUNK)
        quantize_x(1, 0, NT)
        quantize_x(1, NT, CHUNK)
        gate(0, 1)
        products("w", 1, by_half)
        for pair in pairs:
            multiply(0, 0, pair)
            store_y(0, 0, pair)
        products("u", 1, by_place)
        for pair in pairs:
            gate(1, 0, pair)
        multiply(0, 1)
        store_y(0, 1)
        for pair in pairs:
            gate(1, 1, pair)
        round_y(nc.vector.tensor_copy, 0, 0)
        round_y(nc.vector.tensor_copy, 0, 1, 0, POOL_FROM)
        round_y(pool_copy, 0, 1, POOL_FROM, NT)
        for pair in pairs:
            multiply(1, 0, pair)
        store_y(1, 0)
        round_y(nc.scalar.copy, 1, 0)
        for pair in pairs:
            multiply(1, 1, pair)
        store_y(1, 1)
        quantize_y(0, 2)
        round_y(nc.vector.tensor_copy, 1, 1)
        quantize_y(2, 3)
        quantize_y(3, 4)
        for h in range(2):
            store_words(h)
        for h in range(2):
            store_scales(h)
